import numpy as np
import ml_dtypes


def mxq(x, axis, fmt="e4m3"):
    dtype, down = {"e4m3": (ml_dtypes.float8_e4m3fn, 7), "e5m2": (ml_dtypes.float8_e5m2, 14)}[fmt]
    v = np.moveaxis(np.asarray(x, np.float32).astype(ml_dtypes.bfloat16).astype(np.float64), axis, -1)
    blocks = v.reshape(v.shape[:-1] + (-1, 32))
    amax = np.abs(blocks).max(-1, keepdims=True)
    byte = np.maximum(np.where(amax > 0, np.frexp(amax)[1] - 1 + 127, 0) - down, 1)
    scale = np.exp2(byte - 127.0)
    codes = (blocks / scale).astype(np.float32).astype(dtype).astype(np.float64)
    return np.moveaxis((codes * scale).reshape(v.shape), -1, axis)


WIDE = False


def mx_kscale(k):
    if not WIDE:
        return np.ones(k)
    levels = np.array([10, -10, 5, -5, 0])
    if k % 512:
        return np.exp2(np.random.permutation(np.resize(levels, k // 32))).repeat(32)
    a = np.empty((k // 512, 16))
    for p in range(k // 512):
        a[p, :8] = np.random.permutation(np.resize(levels, 8))
        for g in range(8):
            far = levels[np.abs(levels - a[p, g]) >= 10]
            a[p, g + 8] = far[np.random.randint(len(far))]
    return np.exp2(a.ravel()).repeat(32)


BF16 = ml_dtypes.bfloat16


def bf(x):
    return np.asarray(x, np.float32).astype(BF16)


def f64(x):
    return np.asarray(x).astype(np.float64)

def planes(Y):
    n, m = Y.shape
    b = f64(bf(Y)).reshape(n // 32, 32, m)
    amax = np.abs(b).max(1)
    byte = np.clip(np.where(amax > 0, np.frexp(amax)[1] - 1 + 127 - 7, 1), 1, 254)
    codes = (b * np.exp2(127.0 - byte)[:, None, :]).reshape(n, m).astype(np.float32).astype(ml_dtypes.float8_e4m3fn).view(np.uint8)
    words = codes.reshape(n // 512, 128, 4, m).transpose(0, 1, 3, 2)
    return np.ascontiguousarray(words), np.ascontiguousarray(byte.astype(np.uint8).reshape(n // 512, 16, m))


S, A, DK = 2048, 1024, 512


def soft_threshold(u, theta):
    return np.maximum(u - theta, 0.0) - np.maximum(-u - theta, 0.0)


def setup_inputs():
    t = mx_kscale(A)
    s = mx_kscale(DK)
    return {"k": bf(np.random.standard_normal((S, DK)) * s[None, :]),
            "z": bf(np.random.standard_normal((S, A))),
            "a": bf((1.0 + 0.1 * np.random.standard_normal(A)) * t),
            "dic": bf(np.random.standard_normal((A, DK)) / np.sqrt(A) / t[:, None] * s[None, :]),
            "we": bf(np.random.standard_normal((DK, A)) / np.sqrt(DK) / s[:, None]),
            "theta": bf(np.random.uniform(0.2, 0.6, A))}


def core(k, z, a, dic, we, theta):
    z = f64(z)
    za = z * f64(a)[None, :]
    r = f64(k) - (mxq(za, 1, "e4m3") @ mxq(f64(dic), 0, "e4m3"))
    u = z + (mxq(r, 1, "e4m3") @ mxq(f64(we), 0, "e4m3"))
    return soft_threshold(u, f64(theta)[None, :])


def reference(k, z, a, dic, we, theta):
    R_out = core(k, z, a, dic, we, theta)
    words, scales = planes(R_out.T)
    return R_out, words, scales

@@ -1,0 +1,315 @@
+from contextlib import ExitStack
+
+import concourse.mybir as mybir
+from concourse.masks import make_identity
+
+S, A, DK = 2048, 1024, 512
+FLOPS = 4 * S * A * DK
+
+F32 = mybir.dt.float32
+BF16 = mybir.dt.bfloat16
+U32 = mybir.dt.uint32
+I32 = mybir.dt.int32
+U8 = mybir.dt.uint8
+X4 = mybir.dt.float8_e4m3fn_x4
+ALU = mybir.AluOpType
+ACT = mybir.ActivationFunctionType
+
+P = 128
+BANK = 512
+HALF = 256
+CHUNKS = [512, 512, 512, 256, 256]
+
+
+def tile_dictionarykvcachelistastep_x1_kernel(tc, k, z, a, dic, we, theta, out_0, out_1, out_2):
+    nc = tc.nc
+    n = len(CHUNKS)
+    starts = [sum(CHUNKS[:c]) for c in range(n)]
+
+    with ExitStack() as ctx:
+        keep = ctx.enter_context(tc.tile_pool(name="keep", bufs=1))
+        work = ctx.enter_context(tc.tile_pool(name="work", bufs=2))
+        psum = ctx.enter_context(tc.psum_pool(name="psum", bufs=8))
+        ctx.enter_context(tc.manual_schedule())
+
+        def bank():
+            return psum.tile([P, BANK], F32, name="bank")
+
+        ident = keep.tile([P, P], F32, name="ident")
+        make_identity(nc, ident[:])
+
+        a_t = keep.tile([P, 2, 4], BF16, name="a_t")
+        th = keep.tile([P, 2, 4], BF16, name="th")
+        th2 = keep.tile([P, 2, 4], F32, name="th2")
+        nc.scalar.dma_start(out=a_t[:], in_=a.rearrange("(g p t) -> p g t", g=2, t=4))
+        nc.scalar.dma_start(out=th[:], in_=theta.rearrange("(g p t) -> p g t", g=2, t=4))
+
+        z_sb = [keep.tile([P, 2, A], BF16, name="z%d" % h) for h in range(S // HALF)]
+        k_sb = [keep.tile([P, 2, DK], BF16, name="k%d" % h) for h in range(S // HALF)]
+        dic_raw = [keep.tile([P, 4, DK], BF16, name="dicraw%d" % g) for g in range(2)]
+        we_raw = [keep.tile([P, 4, 512], BF16, name="weraw%d" % g) for g in range(2)]
+
+        def load_z(h):
+            nc.sync.dma_start(out=z_sb[h][:], in_=z[h * HALF:(h + 1) * HALF, :].rearrange("(b p) x -> p b x", p=P))
+
+        def load_k(h):
+            nc.sync.dma_start(out=k_sb[h][:], in_=k[h * HALF:(h + 1) * HALF, :].rearrange("(b p) x -> p b x", p=P))
+
+        def load_dic(g):
+            nc.sync.dma_start(out=dic_raw[g][:], in_=dic[g * 512:(g + 1) * 512, :].rearrange("(p j) x -> p j x", j=4))
+
+        def load_we(g):
+            nc.sync.dma_start(out=we_raw[g][:], in_=we[:, g * 512:(g + 1) * 512].rearrange("(p j) x -> p j x", j=4))
+
+        load_dic(0)
+        load_z(0)
+        load_dic(1)
+        load_z(1)
+        load_k(0)
+        load_k(1)
+        load_we(0)
+        load_we(1)
+        for h in range(2, S // HALF, 2):
+            load_z(h)
+            load_z(h + 1)
+            load_k(h)
+            load_k(h + 1)
+
+        nc.scalar.mul(out=th2[:], in_=th[:], mul=-2.0)
+
+        dic_c = keep.tile([P, 2, 512], U32, name="dic_c", align_bytes=64)
+        dic_s = keep.tile([P, 2, 512], U8, name="dic_s", align_bytes=64)
+        we_c = keep.tile([P, 2, 512], U32, name="we_c", align_bytes=64)
+        we_s = keep.tile([P, 2, 512], U8, name="we_s", align_bytes=64)
+        early = starts[n - 1]
+        out_s = [keep.tile([P, 2, early], U8, name="out_s0", align_bytes=64),
+                 keep.tile([P, 2, S - early], U8, name="out_s1", align_bytes=64)]
+
+        def interleave(raw, copy):
+            grouped = work.tile([P, 2048], BF16, name="grouped", align_bytes=64)
+            copy(out=grouped[:].rearrange("p (t m j) -> p t m j", t=4, j=4),
+                 in_=raw[:].rearrange("p j (m t) -> p t m j", t=4))
+            return grouped
+
+        def quant(codes, scales, src):
+            nc.vector.quantize_mx(out=codes.bitcast(X4), scales=scales, in_=src)
+
+        zt, kt, za, zc, zs, rb, rc, rs = {}, {}, {}, {}, {}, {}, {}, {}
+        zbank, m1bank, m2bank, wt, at, ot, ob = {}, {}, {}, {}, {}, {}, {}
+
+        def halves(c):
+            return range(CHUNKS[c] // HALF)
+
+        def transpose_words(src, col0):
+            pb = bank()
+            words = src[:].bitcast(F32)
+            for u in range(2):
+                for b in range(2):
+                    nc.tensor.transpose(pb[:, u * HALF + b * P:u * HALF + (b + 1) * P],
+                                        words[:, b, col0 + u:col0 + 256:2], ident[:])
+            return pb
+
+        def tz(c, h):
+            for g in range(2):
+                zbank[c, h, g] = transpose_words(z_sb[starts[c] // HALF + h], 256 * g)
+
+        def za_ez(c, h):
+            if h == 0:
+                zt[c] = work.tile([P, 2, 2, 512], F32, name="zt")
+                za[c] = work.tile([P, 2, 2048], BF16, name="za", bufs=1, align_bytes=64)
+            for g in range(2):
+                pb = zbank[c, h, g]
+                nc.vector.tensor_tensor(
+                    out=za[c][:, g, h * 4 * HALF:(h + 1) * 4 * HALF].rearrange("p (r u e) -> p r u e", u=2, e=2),
+                    in0=pb[:].bitcast(BF16).rearrange("p (u r e) -> p r u e", u=2, e=2),
+                    in1=a_t[:, g:g + 1, :].rearrange("p o (u e) -> p o u e", u=2).to_broadcast([P, HALF, 2, 2]),
+                    op=ALU.mult)
+                nc.scalar.copy(out=zt[c][:, g, :, h * HALF:(h + 1) * HALF], in_=pb[:].rearrange("p (u r) -> p u r", u=2))
+
+        def qz(c):
+            w = CHUNKS[c]
+            zc[c] = work.tile([P, 2, 512], U32, name="zc", align_bytes=64)
+            zs[c] = work.tile([P, 2, 512], U8, name="zs", align_bytes=64)
+            for g in range(2):
+                quant(zc[c][:, g, :w], zs[c][:, g, :w], za[c][:, g, :4 * w])
+
+        def tk_ek(c):
+            kt[c] = work.tile([P, 512, 2], F32, name="kt")
+            banks = [transpose_words(k_sb[starts[c] // HALF + h], 0) for h in halves(c)]
+            for h in halves(c):
+                nc.scalar.copy(out=kt[c][:, h * HALF:(h + 1) * HALF, :], in_=banks[h][:].rearrange("p (u r) -> p r u", u=2))
+
+        def mm1(c):
+            for b in range(CHUNKS[c] // P):
+                pb = bank()
+                m1bank[c, b] = pb
+                for t in range(4):
+                    for g in range(2):
+                        nc.tensor.matmul_mx(
+                            out=pb[:, t * P:(t + 1) * P],
+                            lhsT=dic_c[:, g, t * P:(t + 1) * P].bitcast(X4), lhsT_scale=dic_s[:, g, t * P:(t + 1) * P],
+                            rhs=zc[c][:, g, b * P:(b + 1) * P].bitcast(X4), rhs_scale=zs[c][:, g, b * P:(b + 1) * P],
+                            start=(g == 0), stop=(g == 1))
+
+        def residual(c):
+            rb[c] = work.tile([P, 2048], BF16, name="rb", bufs=1, align_bytes=64)
+            kb = kt[c][:].rearrange("p r u -> p (r u)").bitcast(BF16)
+            for b in range(CHUNKS[c] // P):
+                cols = slice(b * 512, (b + 1) * 512)
+                nc.vector.tensor_tensor(
+                    out=rb[c][:, cols].rearrange("p (r t) -> p r t", t=4),
+                    in0=kb[:, cols].rearrange("p (r t) -> p r t", t=4),
+                    in1=m1bank[c, b][:].rearrange("p (t r) -> p r t", t=4),
+                    op=ALU.subtract)
+
+        def qr(c):
+            w = CHUNKS[c]
+            rc[c] = work.tile([P, 512], U32, name="rc", align_bytes=64)
+            rs[c] = work.tile([P, 512], U8, name="rs", align_bytes=64)
+            quant(rc[c][:, :w], rs[c][:, :w], rb[c][:, :4 * w])
+
+        def mm2(c, g):
+            w = CHUNKS[c]
+            per = BANK // w
+            for t in range(4):
+                if t % per == 0:
+                    pb = bank()
+                m2bank[c, g, t] = pb[:, (t % per) * w:(t % per + 1) * w]
+                nc.tensor.matmul_mx(
+                    out=m2bank[c, g, t],
+                    lhsT=we_c[:, g, t * P:(t + 1) * P].bitcast(X4), lhsT_scale=we_s[:, g, t * P:(t + 1) * P],
+                    rhs=rc[c][:, :w].bitcast(X4), rhs_scale=rs[c][:, :w], start=True, stop=True)
+
+        def shift(c, g):
+            w = CHUNKS[c]
+            wt[c, g] = work.tile([P, 4, 512], F32, name="wt")
+            at[c, g] = work.tile([P, 4, 512], F32, name="at")
+            for t in range(4):
+                zb = zt[c][:, g, t // 2, :w].bitcast(BF16).rearrange("p (r e) -> p r e", e=2)[:, :, t % 2]
+                nc.vector.scalar_tensor_tensor(out=wt[c, g][:, t, :w], in0=m2bank[c, g, t], scalar=th[:, g, t:t + 1],
+                                               in1=zb, op0=ALU.add, op1=ALU.add)
+                nc.scalar.activation(out=at[c, g][:, t, :w], in_=wt[c, g][:, t, :w], func=ACT.Relu,
+                                     bias=th2[:, g, t:t + 1])
+
+        def combine(c, g):
+            w = CHUNKS[c]
+            ot[c, g] = work.tile([P, 4, 512], F32, name="ot")
+            nc.vector.scalar_tensor_tensor(out=ot[c, g][:, :, :w], in0=wt[c, g][:, :, :w], scalar=0.0,
+                                           in1=at[c, g][:, :, :w], op0=ALU.min, op1=ALU.add)
+
+        def cast(c, g):
+            w = CHUNKS[c]
+            ob[c, g] = work.tile([P, 2048], BF16, name="ob", align_bytes=64)
+            dst = ob[c, g][:, :4 * w].rearrange("p (r t) -> p r t", t=4)
+            src = ot[c, g][:, :, :w].rearrange("p t r -> p r t")
+            if c == n - 1 and g == 1:
+                nc.vector.tensor_copy(out=dst, in_=src)
+            else:
+                nc.gpsimd.tensor_scalar(out=dst, in0=src, scalar1=1.0, scalar2=0.0, op0=ALU.mult, op1=ALU.add)
+
+        def qo(c, g):
+            w = CHUNKS[c]
+            oc = work.tile([P, 512], U32, name="oc", align_bytes=64)
+            plane = out_s[1][:, g, :] if c == n - 1 else out_s[0][:, g, starts[c]:starts[c] + w]
+            quant(oc[:, :w], plane, ob[c, g][:, :4 * w])
+            nc.sync.dma_start(out=out_1[g].rearrange("p m t -> p (m t)").bitcast(I32)[:, starts[c]:starts[c] + w],
+                              in_=oc[:, :w].bitcast(I32))
+
+        def to_eo(c, g):
+            nb = CHUNKS[c] // P
+            res = work.tile([P, 4, 512], F32, name="res", bufs=3)
+            for b in range(nb):
+                pb = bank()
+                for t in range(4):
+                    nc.tensor.transpose(pb[:, t * P:(t + 1) * P], ot[c, g][:, t, b * P:(b + 1) * P], ident[:])
+                nc.scalar.copy(out=res[:, b, :].rearrange("p (m t) -> p m t", t=4),
+                               in_=pb[:].rearrange("p (t m) -> p m t", t=4))
+            nc.sync.dma_start(
+                out=out_0[starts[c]:starts[c] + CHUNKS[c], g * 512:(g + 1) * 512].rearrange("(b p) x -> p b x", p=P),
+                in_=res[:, :nb, :])
+
+        def store_scales(part, m0, m1):
+            for q in range(4):
+                nc.sync.dma_start(
+                    out=out_2.bitcast(I32)[:, 4 * q:4 * q + 4, m0 // 4:m1 // 4].rearrange("g r m -> r g m"),
+                    in_=out_s[part][:].bitcast(I32)[32 * q:32 * q + 4, :, :])
+
+        gd0 = interleave(dic_raw[0], nc.vector.tensor_copy)
+        gd1 = interleave(dic_raw[1], nc.scalar.copy)
+        tz(0, 0)
+        za_ez(0, 0)
+        quant(dic_c[:, 0, :], dic_s[:, 0, :], gd0[:])
+        for h in halves(0)[1:]:
+            tz(0, h)
+            za_ez(0, h)
+        quant(dic_c[:, 1, :], dic_s[:, 1, :], gd1[:])
+        qz(0)
+        tk_ek(0)
+        mm1(0)
+        gw0 = interleave(we_raw[0], nc.vector.tensor_copy)
+        gw1 = interleave(we_raw[1], nc.scalar.copy)
+        residual(0)
+        quant(we_c[:, 0, :], we_s[:, 0, :], gw0[:])
+        qr(0)
+        tk_ek(1)
+        mm2(0, 0)
+        quant(we_c[:, 1, :], we_s[:, 1, :], gw1[:])
+
+        for i in range(n):
+            more = i + 1 < n
+            if more:
+                for h in halves(i + 1):
+                    tz(i + 1, h)
+            shift(i, 0)
+            if more:
+                for h in halves(i + 1):
+                    za_ez(i + 1, h)
+            if i > 0:
+                to_eo(i - 1, 1)
+            if more:
+                qz(i + 1)
+            if i > 0 and CHUNKS[min(i + 1, n - 1)] == 512:
+                qo(i - 1, 1)
+            mm2(i, 1)
+            if more:
+                mm1(i + 1)
+            combine(i, 0)
+            if i > 0 and CHUNKS[min(i + 1, n - 1)] != 512:
+                qo(i - 1, 1)
+            if not more:
+                store_scales(0, 0, early)
+            cast(i, 0)
+            shift(i, 1)
+            to_eo(i, 0)
+            if more:
+                residual(i + 1)
+            if more:
+                qo(i, 0)
+                qr(i + 1)
+            if i + 2 < n:
+                tk_ek(i + 2)
+            if more:
+                mm2(i + 1, 0)
+            if more:
+                combine(i, 1)
+                cast(i, 1)
+        c = n - 1
+        w = CHUNKS[c]
+        ot[c, 1] = work.tile([P, 4, 512], F32, name="ot")
+        res = work.tile([P, 4, 512], F32, name="res", bufs=3)
+        for b in range(w // P):
+            blk = slice(b * P, (b + 1) * P)
+            nc.vector.scalar_tensor_tensor(out=ot[c, 1][:, :, blk], in0=wt[c, 1][:, :, blk], scalar=0.0,
+                                           in1=at[c, 1][:, :, blk], op0=ALU.min, op1=ALU.add)
+        qo(c, 0)
+        for b in range(w // P):
+            blk = slice(b * P, (b + 1) * P)
+            pb = bank()
+            for t in range(4):
+                nc.tensor.transpose(pb[:, t * P:(t + 1) * P], ot[c, 1][:, t, blk], ident[:])
+            nc.scalar.copy(out=res[:, b, :].rearrange("p (m t) -> p m t", t=4),
+                           in_=pb[:].rearrange("p (t m) -> p m t", t=4))
+            nc.sync.dma_start(out=out_0[starts[c] + b * P:starts[c] + (b + 1) * P, 512:1024], in_=res[:, b, :])
+        cast(c, 1)
+        qo(c, 1)
+        store_scales(1, early, S)

@@ -18,7 +18,15 @@ ACT = mybir.ActivationFunctionType
 P = 128
 BANK = 512
 HALF = 256
-CHUNKS = [512, 512, 512, 256, 256]
+CHUNKS = [256, 512, 512, 512, 256]
+ORDER = [('tz', 0, 0, 0), ('il', 'd', 1, 1), ('il', 'd', 0, 1), ('il', 'd', 1, 0), ('il', 'd', 0, 0), ('qw', 'd', 0), ('tz', 0, 0, 1), ('il', 'w', 0, 1), ('za', 0, 0, 0), ('tk', 0, 0), ('il', 'w', 0, 0), ('za', 0, 0, 1), ('qw', 'd', 1), ('qz', 0), ('mm1', 0, 0), ('ek', 0, 0), ('mm1', 0, 1), ('tk', 1, 1), ('il', 'w', 1, 0), ('tk', 1, 0), ('evp', 0, 0), ('tr', 0, 0), ('il', 'w', 1, 1), ('evp', 0, 1), ('tr', 0, 1), ('qw', 'w', 0), ('ez', 0, 0, 0), ('rs', 0, 0), ('rs', 0, 1), ('qr', 0), ('tz', 1, 0, 0), ('ez', 0, 0, 1), ('mm2', 0, 0, 1), ('qw', 'w', 1), ('ev', 0, 0, 2), ('za', 1, 0, 0), ('ev', 0, 0, 3), ('mm2', 0, 0, 0), ('p1', 0, 0, 3), ('ez', 1, 0, 0), ('ev', 0, 0, 1), ('ev', 0, 0, 0), ('ek', 1, 1), ('p1', 0, 0, 0), ('tz', 1, 0, 1), ('tz', 1, 1, 1), ('ez', 1, 1, 1), ('ek', 1, 0), ('tz', 1, 1, 0), ('p1', 0, 0, 1), ('mm2', 0, 1, 0), ('ev', 0, 1, 1), ('ev', 0, 1, 0), ('relu', 0, 0, 1), ('p1', 0, 0, 2), ('relu', 0, 0, 2), ('za', 1, 0, 1), ('za', 1, 1, 0), ('za', 1, 1, 1), ('qz', 1), ('relu', 0, 0, 0), ('mm2', 0, 1, 1), ('ez', 1, 1, 0), ('mm1', 1, 3), ('mm1', 1, 1), ('relu', 0, 0, 3), ('mm1', 1, 2), ('p1', 0, 1, 0), ('ez', 1, 0, 1), ('p1', 0, 1, 1), ('p3', 0, 0, 0), ('mm1', 1, 0), ('ev', 0, 1, 2), ('evp', 1, 2), ('p1', 0, 1, 2), ('p3', 0, 0, 1), ('evp', 1, 3), ('evp', 1, 0), ('tr', 1, 3), ('evp', 1, 1), ('tr', 1, 2), ('rs', 1, 3), ('relu', 0, 1, 1), ('relu', 0, 1, 2), ('tr', 1, 0), ('ev', 0, 1, 3), ('tr', 1, 1), ('to', 0, 0, 0), ('relu', 0, 1, 0), ('rs', 1, 1), ('eo', 0, 0, 0), ('cast', 0, 0, 1), ('rs', 1, 2), ('rs', 1, 0), ('p1', 0, 1, 3), ('relu', 0, 1, 3), ('to', 0, 0, 1), ('tk', 2, 1), ('eo', 0, 0, 1), ('cast', 0, 0, 0), ('qr', 1), ('qo', 0, 0), ('p3', 0, 1, 1), ('tk', 2, 0), ('mm2', 1, 0, 2), ('mm2', 1, 0, 1), ('p3', 0, 1, 0), ('ek', 2, 1), ('mm2', 1, 0, 0), ('cast', 0, 1, 1), ('mm2', 1, 0, 3), ('ek', 2, 0), ('cast', 0, 1, 0), ('ev', 1, 0, 0), ('ev', 1, 0, 1), ('p1', 1, 0, 1), ('ev', 1, 0, 2), ('tz', 2, 0, 0), ('tz', 2, 1, 0), ('p1', 1, 0, 2), ('tz', 2, 0, 1), ('p1', 1, 0, 0), ('za', 2, 0, 0), ('ez', 2, 1, 0), ('ev', 1, 0, 3), ('tz', 2, 1, 1), ('relu', 1, 0, 0), ('mm2', 1, 1, 2), ('relu', 1, 0, 2), ('p1', 1, 0, 3), ('za', 2, 0, 1), ('ev', 1, 1, 2), ('mm2', 1, 1, 0), ('za', 2, 1, 0), ('mm2', 1, 1, 1), ('ez', 2, 0, 0), ('relu', 1, 0, 3), ('ez', 2, 0, 1), ('ev', 1, 1, 0), ('za', 2, 1, 1), ('qz', 2), ('qo', 0, 1), ('to', 0, 1, 0), ('relu', 1, 0, 1), ('mm2', 1, 1, 3), ('mm1', 2, 0), ('to', 0, 1, 1), ('ev', 1, 1, 1), ('ev', 1, 1, 3), ('p3', 1, 0, 0), ('p3', 1, 0, 1), ('eo', 0, 1, 0), ('evp', 2, 0), ('p1', 1, 1, 2), ('ez', 2, 1, 1), ('p1', 1, 1, 0), ('mm1', 2, 1), ('mm1', 2, 2), ('mm1', 2, 3), ('p1', 1, 1, 1), ('evp', 2, 2), ('evp', 2, 3), ('cast', 1, 0, 1), ('evp', 2, 1), ('cast', 1, 0, 0), ('eo', 0, 1, 1), ('to', 1, 0, 0), ('p1', 1, 1, 3), ('tr', 2, 0), ('tr', 2, 1), ('tr', 2, 2), ('to', 1, 0, 2), ('rs', 2, 0), ('relu', 1, 1, 2), ('relu', 1, 1, 1), ('rs', 2, 1), ('relu', 1, 1, 3), ('tk', 3, 1), ('rs', 2, 2), ('relu', 1, 1, 0), ('eo', 1, 0, 0), ('tk', 3, 0), ('to', 1, 0, 1), ('eo', 1, 0, 2), ('tr', 2, 3), ('rs', 2, 3), ('qo', 1, 0), ('qr', 2), ('to', 1, 0, 3), ('mm2', 2, 0, 2), ('ek', 3, 1), ('p3', 1, 1, 1), ('p3', 1, 1, 0), ('ek', 3, 0), ('mm2', 2, 0, 1), ('mm2', 2, 0, 0), ('eo', 1, 0, 1), ('eo', 1, 0, 3), ('cast', 1, 1, 1), ('cast', 1, 1, 0), ('mm2', 2, 0, 3), ('to', 1, 1, 2), ('ev', 2, 0, 0), ('ev', 2, 0, 1), ('p1', 2, 0, 1), ('ev', 2, 0, 2), ('tz', 3, 0, 0), ('tz', 3, 1, 0), ('p1', 2, 0, 2), ('tz', 3, 0, 1), ('p1', 2, 0, 0), ('to', 1, 1, 3), ('eo', 1, 1, 2), ('za', 3, 0, 0), ('ez', 3, 1, 0), ('ev', 2, 0, 3), ('tz', 3, 1, 1), ('relu', 2, 0, 0), ('mm2', 2, 1, 2), ('relu', 2, 0, 2), ('p1', 2, 0, 3), ('za', 3, 0, 1), ('ev', 2, 1, 2), ('mm2', 2, 1, 0), ('za', 3, 1, 0), ('mm2', 2, 1, 1), ('ez', 3, 0, 0), ('relu', 2, 0, 3), ('eo', 1, 1, 3), ('ez', 3, 0, 1), ('ev', 2, 1, 0), ('za', 3, 1, 1), ('qz', 3), ('qo', 1, 1), ('to', 1, 1, 0), ('relu', 2, 0, 1), ('mm2', 2, 1, 3), ('mm1', 3, 0), ('to', 1, 1, 1), ('ev', 2, 1, 1), ('ev', 2, 1, 3), ('p3', 2, 0, 0), ('p3', 2, 0, 1), ('eo', 1, 1, 0), ('evp', 3, 0), ('p1', 2, 1, 2), ('ez', 3, 1, 1), ('p1', 2, 1, 0), ('mm1', 3, 1), ('mm1', 3, 2), ('mm1', 3, 3), ('p1', 2, 1, 1), ('evp', 3, 2), ('evp', 3, 3), ('cast', 2, 0, 1), ('evp', 3, 1), ('cast', 2, 0, 0), ('eo', 1, 1, 1), ('to', 2, 0, 0), ('p1', 2, 1, 3), ('tr', 3, 0), ('tr', 3, 1), ('tr', 3, 2), ('to', 2, 0, 2), ('rs', 3, 0), ('relu', 2, 1, 2), ('relu', 2, 1, 1), ('rs', 3, 1), ('relu', 2, 1, 3), ('rs', 3, 2), ('relu', 2, 1, 0), ('eo', 2, 0, 0), ('tk', 4, 0), ('to', 2, 0, 1), ('eo', 2, 0, 2), ('tr', 3, 3), ('rs', 3, 3), ('qo', 2, 0), ('qr', 3), ('to', 2, 0, 3), ('mm2', 3, 0, 2), ('p3', 2, 1, 1), ('p3', 2, 1, 0), ('ek', 4, 0), ('mm2', 3, 0, 1), ('mm2', 3, 0, 0), ('eo', 2, 0, 1), ('eo', 2, 0, 3), ('cast', 2, 1, 1), ('cast', 2, 1, 0), ('mm2', 3, 0, 3), ('to', 2, 1, 2), ('ev', 3, 0, 0), ('ev', 3, 0, 1), ('p1', 3, 0, 1), ('ev', 3, 0, 2), ('tz', 4, 0, 0), ('p1', 3, 0, 2), ('tz', 4, 0, 1), ('p1', 3, 0, 0), ('to', 2, 1, 3), ('eo', 2, 1, 2), ('za', 4, 0, 0), ('ev', 3, 0, 3), ('relu', 3, 0, 0), ('mm2', 3, 1, 2), ('relu', 3, 0, 2), ('p1', 3, 0, 3), ('za', 4, 0, 1), ('ev', 3, 1, 2), ('mm2', 3, 1, 0), ('mm2', 3, 1, 1), ('ez', 4, 0, 0), ('relu', 3, 0, 3), ('eo', 2, 1, 3), ('ez', 4, 0, 1), ('ev', 3, 1, 0), ('qz', 4), ('qo', 2, 1), ('to', 2, 1, 0), ('relu', 3, 0, 1), ('mm2', 3, 1, 3), ('mm1', 4, 0), ('to', 2, 1, 1), ('ev', 3, 1, 1), ('ev', 3, 1, 3), ('p3', 3, 0, 0), ('p3', 3, 0, 1), ('eo', 2, 1, 0), ('evp', 4, 0), ('p1', 3, 1, 2), ('p1', 3, 1, 0), ('mm1', 4, 1), ('p1', 3, 1, 1), ('cast', 3, 0, 1), ('evp', 4, 1), ('cast', 3, 0, 0), ('eo', 2, 1, 1), ('to', 3, 0, 0), ('p1', 3, 1, 3), ('tr', 4, 0), ('tr', 4, 1), ('to', 3, 0, 2), ('rs', 4, 0), ('relu', 3, 1, 2), ('relu', 3, 1, 1), ('rs', 4, 1), ('relu', 3, 1, 3), ('relu', 3, 1, 0), ('eo', 3, 0, 0), ('to', 3, 0, 1), ('eo', 3, 0, 2), ('qo', 3, 0), ('qr', 4), ('to', 3, 0, 3), ('p3', 3, 1, 1), ('p3', 3, 1, 0), ('mm2', 4, 0, 1), ('mm2', 4, 0, 0), ('eo', 3, 0, 1), ('eo', 3, 0, 3), ('cast', 3, 1, 1), ('cast', 3, 1, 0), ('ev', 4, 0, 3), ('mm2', 4, 1, 0), ('mm2', 4, 1, 1), ('to', 3, 1, 0), ('ev', 4, 0, 1), ('ev', 4, 1, 0), ('p1', 4, 0, 1), ('ev', 4, 0, 0), ('p1', 4, 0, 3), ('ev', 4, 1, 2), ('relu', 4, 0, 1), ('to', 3, 1, 3), ('p1', 4, 0, 0), ('p1', 4, 1, 2), ('ev', 4, 0, 2), ('relu', 4, 0, 3), ('eo', 3, 1, 0), ('to', 3, 1, 1), ('ev', 4, 1, 3), ('to', 3, 1, 2), ('p1', 4, 1, 0), ('p1', 4, 0, 2), ('relu', 4, 0, 0), ('ev', 4, 1, 1), ('relu', 4, 1, 2), ('p1', 4, 1, 1), ('relu', 4, 0, 2), ('eo', 3, 1, 2), ('p1', 4, 1, 3), ('eo', 3, 1, 1), ('eo', 3, 1, 3), ('p3', 4, 0, 0), ('p3', 4, 0, 1), ('qo', 3, 1), ('ss', 0), ('relu', 4, 1, 3), ('to', 4, 0, 0), ('relu', 4, 1, 1), ('to', 4, 0, 1), ('relu', 4, 1, 0), ('eo', 4, 0, 0), ('p3', 4, 1, 0), ('eo', 4, 0, 1), ('p3', 4, 1, 1), ('to', 4, 1, 0), ('cast', 4, 1, 1), ('cast', 4, 0, 0), ('to', 4, 1, 1), ('eo', 4, 1, 0), ('eo', 4, 1, 1), ('cast', 4, 1, 0), ('cast', 4, 0, 1), ('qo', 4, 0), ('qo', 4, 1), ('ss', 1)]
+LOADS = [('d', 0), ('d', 1), ('z', 0), ('k', 0), ('w', 0), ('k', 2), ('k', 3), ('w', 1), ('k', 1), ('z', 1), ('z', 2), ('z', 3), ('z', 4), ('k', 4), ('z', 5), ('k', 5), ('z', 6), ('k', 6), ('z', 7), ('k', 7)]
+CAST = {(0, 0, 0): 'g', (0, 0, 1): 'g', (0, 1, 0): 'g', (0, 1, 1): 'g', (1, 0, 0): 's', (1, 0, 1): 'g', (1, 1, 0): 's', (1, 1, 1): 'g', (2, 0, 0): 's', (2, 0, 1): 'g', (2, 1, 0): 's', (2, 1, 1): 'g', (3, 0, 0): 's', (3, 0, 1): 'g', (3, 1, 0): 'g', (3, 1, 1): 's', (4, 0, 0): 'g', (4, 0, 1): 's', (4, 1, 0): 'v', (4, 1, 1): 's'}
+EOV = {(3, 1, 3), (4, 1, 0), (4, 1, 1), (3, 1, 1)}
+OFF = {(2, 1, 0), (3, 1, 0), (1, 1, 0)}
+RELUG = {(1, 0, 1), (2, 0, 2), (2, 0, 1), (3, 0, 2), (3, 0, 1), (1, 0, 2)}
+RPE = set()
+IL = {('d', 0, 0): 'v', ('d', 0, 1): 'v', ('d', 1, 0): 'v', ('d', 1, 1): 's', ('w', 0, 0): 's', ('w', 0, 1): 's', ('w', 1, 0): 'v', ('w', 1, 1): 's'}
 
 
 def tile_dictionarykvcachelistastep_x1_kernel(tc, k, z, a, dic, we, theta, out_0, out_1, out_2):
@@ -29,14 +37,19 @@ def tile_dictionarykvcachelistastep_x1_kernel(tc, k, z, a, dic, we, theta, out_0
     with ExitStack() as ctx:
         keep = ctx.enter_context(tc.tile_pool(name="keep", bufs=1))
         work = ctx.enter_context(tc.tile_pool(name="work", bufs=2))
-        psum = ctx.enter_context(tc.psum_pool(name="psum", bufs=8))
+        psum = ctx.enter_context(tc.psum_pool(name="psum", bufs=1))
         ctx.enter_context(tc.manual_schedule())
 
+        used = []
+
         def bank():
-            return psum.tile([P, BANK], F32, name="bank")
+            used.append(len(used) % 8)
+            return psum.tile([P, BANK], F32, name="bank%d" % used[-1])
 
         ident = keep.tile([P, P], F32, name="ident")
         make_identity(nc, ident[:])
+        ident_b = keep.tile([P, P], BF16, name="ident_b")
+        make_identity(nc, ident_b[:])
 
         a_t = keep.tile([P, 2, 4], BF16, name="a_t")
         th = keep.tile([P, 2, 4], BF16, name="th")
@@ -61,19 +74,9 @@ def tile_dictionarykvcachelistastep_x1_kernel(tc, k, z, a, dic, we, theta, out_0
         def load_we(g):
             nc.sync.dma_start(out=we_raw[g][:], in_=we[:, g * 512:(g + 1) * 512].rearrange("(p j) x -> p j x", j=4))
 
-        load_dic(0)
-        load_z(0)
-        load_dic(1)
-        load_z(1)
-        load_k(0)
-        load_k(1)
-        load_we(0)
-        load_we(1)
-        for h in range(2, S // HALF, 2):
-            load_z(h)
-            load_z(h + 1)
-            load_k(h)
-            load_k(h + 1)
+        loads = {"d": load_dic, "z": load_z, "k": load_k, "w": load_we}
+        for name, j in LOADS:
+            loads[name](j)
 
         nc.scalar.mul(out=th2[:], in_=th[:], mul=-2.0)
 
@@ -85,16 +88,11 @@ def tile_dictionarykvcachelistastep_x1_kernel(tc, k, z, a, dic, we, theta, out_0
         out_s = [keep.tile([P, 2, early], U8, name="out_s0", align_bytes=64),
                  keep.tile([P, 2, S - early], U8, name="out_s1", align_bytes=64)]
 
-        def interleave(raw, copy):
-            grouped = work.tile([P, 2048], BF16, name="grouped", align_bytes=64)
-            copy(out=grouped[:].rearrange("p (t m j) -> p t m j", t=4, j=4),
-                 in_=raw[:].rearrange("p j (m t) -> p t m j", t=4))
-            return grouped
-
         def quant(codes, scales, src):
             nc.vector.quantize_mx(out=codes.bitcast(X4), scales=scales, in_=src)
 
         zt, kt, za, zc, zs, rb, rc, rs = {}, {}, {}, {}, {}, {}, {}, {}
+        kbank, obank, rest, grp, w0, neg, rbank = {}, {}, {}, {}, {}, {}, {}
         zbank, m1bank, m2bank, wt, at, ot, ob = {}, {}, {}, {}, {}, {}, {}
 
         def halves(c):
@@ -103,28 +101,29 @@ def tile_dictionarykvcachelistastep_x1_kernel(tc, k, z, a, dic, we, theta, out_0
         def transpose_words(src, col0):
             pb = bank()
             words = src[:].bitcast(F32)
-            for u in range(2):
-                for b in range(2):
+            for b in range(2):
+                for u in range(2):
                     nc.tensor.transpose(pb[:, u * HALF + b * P:u * HALF + (b + 1) * P],
                                         words[:, b, col0 + u:col0 + 256:2], ident[:])
             return pb
 
-        def tz(c, h):
-            for g in range(2):
-                zbank[c, h, g] = transpose_words(z_sb[starts[c] // HALF + h], 256 * g)
+        def tz(c, h, g):
+            zbank[c, h, g] = transpose_words(z_sb[starts[c] // HALF + h], 256 * g)
 
-        def za_ez(c, h):
-            if h == 0:
-                zt[c] = work.tile([P, 2, 2, 512], F32, name="zt")
+        def za_(c, h, g):
+            if c not in za:
                 za[c] = work.tile([P, 2, 2048], BF16, name="za", bufs=1, align_bytes=64)
-            for g in range(2):
-                pb = zbank[c, h, g]
-                nc.vector.tensor_tensor(
-                    out=za[c][:, g, h * 4 * HALF:(h + 1) * 4 * HALF].rearrange("p (r u e) -> p r u e", u=2, e=2),
-                    in0=pb[:].bitcast(BF16).rearrange("p (u r e) -> p r u e", u=2, e=2),
-                    in1=a_t[:, g:g + 1, :].rearrange("p o (u e) -> p o u e", u=2).to_broadcast([P, HALF, 2, 2]),
-                    op=ALU.mult)
-                nc.scalar.copy(out=zt[c][:, g, :, h * HALF:(h + 1) * HALF], in_=pb[:].rearrange("p (u r) -> p u r", u=2))
+            nc.vector.tensor_tensor(
+                out=za[c][:, g, h * 4 * HALF:(h + 1) * 4 * HALF].rearrange("p (r u e) -> p r u e", u=2, e=2),
+                in0=zbank[c, h, g][:].bitcast(BF16).rearrange("p (u r e) -> p r u e", u=2, e=2),
+                in1=a_t[:, g:g + 1, :].rearrange("p o (u e) -> p o u e", u=2).to_broadcast([P, HALF, 2, 2]),
+                op=ALU.mult)
+
+        def ez(c, h, g):
+            if c not in zt:
+                zt[c] = work.tile([P, 2, 2, 512], F32, name="zt")
+            nc.scalar.copy(out=zt[c][:, g, :, h * HALF:(h + 1) * HALF],
+                           in_=zbank[c, h, g][:].rearrange("p (u r) -> p u r", u=2))
 
         def qz(c):
             w = CHUNKS[c]
@@ -133,34 +132,66 @@ def tile_dictionarykvcachelistastep_x1_kernel(tc, k, z, a, dic, we, theta, out_0
             for g in range(2):
                 quant(zc[c][:, g, :w], zs[c][:, g, :w], za[c][:, g, :4 * w])
 
-        def tk_ek(c):
-            kt[c] = work.tile([P, 512, 2], F32, name="kt")
-            banks = [transpose_words(k_sb[starts[c] // HALF + h], 0) for h in halves(c)]
-            for h in halves(c):
-                nc.scalar.copy(out=kt[c][:, h * HALF:(h + 1) * HALF, :], in_=banks[h][:].rearrange("p (u r) -> p r u", u=2))
+        def tk(c, h):
+            if (c, h) in RPE:
+                return
+            kbank[c, h] = transpose_words(k_sb[starts[c] // HALF + h], 0)
 
-        def mm1(c):
-            for b in range(CHUNKS[c] // P):
+        def ek(c, h):
+            if (c, h) in RPE:
+                return
+            if c not in kt:
+                kt[c] = work.tile([P, 512, 2], F32, name="kt")
+            nc.scalar.copy(out=kt[c][:, h * HALF:(h + 1) * HALF, :], in_=kbank[c, h][:].rearrange("p (u r) -> p r u", u=2))
+
+        def mm1(c, b):
+            pb = bank()
+            m1bank[c, b] = pb
+            if (c, b // 2) in RPE:
+                for g in range(2):
+                    nc.tensor.matmul_mx(
+                        out=pb[:], lhsT=zc[c][:, g, b * P:(b + 1) * P].bitcast(X4),
+                        lhsT_scale=zs[c][:, g, b * P:(b + 1) * P],
+                        rhs=dic_c[:, g, :].bitcast(X4), rhs_scale=dic_s[:, g, :], start=(g == 0), stop=(g == 1))
+                return
+            for t in range(4):
+                for g in range(2):
+                    nc.tensor.matmul_mx(
+                        out=pb[:, t * P:(t + 1) * P],
+                        lhsT=dic_c[:, g, t * P:(t + 1) * P].bitcast(X4), lhsT_scale=dic_s[:, g, t * P:(t + 1) * P],
+                        rhs=zc[c][:, g, b * P:(b + 1) * P].bitcast(X4), rhs_scale=zs[c][:, g, b * P:(b + 1) * P],
+                        start=(g == 0), stop=(g == 1))
+
+        def evp(c, b):
+            if (c, b // 2) in RPE:
+                neg[c, b] = work.tile([P, 512], F32, name="neg")
+                nc.scalar.mul(out=neg[c, b][:], in_=m1bank[c, b][:], mul=-1.0)
+
+        def tr(c, b):
+            if (c, b // 2) in RPE:
                 pb = bank()
-                m1bank[c, b] = pb
+                rbank[c, b] = pb
+                rows = k_sb[starts[c] // HALF + b // 2]
                 for t in range(4):
-                    for g in range(2):
-                        nc.tensor.matmul_mx(
-                            out=pb[:, t * P:(t + 1) * P],
-                            lhsT=dic_c[:, g, t * P:(t + 1) * P].bitcast(X4), lhsT_scale=dic_s[:, g, t * P:(t + 1) * P],
-                            rhs=zc[c][:, g, b * P:(b + 1) * P].bitcast(X4), rhs_scale=zs[c][:, g, b * P:(b + 1) * P],
-                            start=(g == 0), stop=(g == 1))
+                    nc.tensor.matmul(pb[:, t * P:(t + 1) * P], lhsT=rows[:, b % 2, t:DK:4], rhs=ident_b[:],
+                                     start=True, stop=False)
+                    nc.tensor.matmul(pb[:, t * P:(t + 1) * P], lhsT=neg[c, b][:, t * P:(t + 1) * P], rhs=ident[:],
+                                     start=False, stop=True, is_transpose=True)
 
-        def residual(c):
-            rb[c] = work.tile([P, 2048], BF16, name="rb", bufs=1, align_bytes=64)
+        def res_(c, b):
+            if c not in rb:
+                rb[c] = work.tile([P, 2048], BF16, name="rb", bufs=1, align_bytes=64)
+            if (c, b // 2) in RPE:
+                nc.scalar.copy(out=rb[c][:, b * 512:(b + 1) * 512].rearrange("p (r t) -> p r t", t=4),
+                               in_=rbank[c, b][:].rearrange("p (t r) -> p r t", t=4))
+                return
             kb = kt[c][:].rearrange("p r u -> p (r u)").bitcast(BF16)
-            for b in range(CHUNKS[c] // P):
-                cols = slice(b * 512, (b + 1) * 512)
-                nc.vector.tensor_tensor(
-                    out=rb[c][:, cols].rearrange("p (r t) -> p r t", t=4),
-                    in0=kb[:, cols].rearrange("p (r t) -> p r t", t=4),
-                    in1=m1bank[c, b][:].rearrange("p (t r) -> p r t", t=4),
-                    op=ALU.subtract)
+            cols = slice(b * 512, (b + 1) * 512)
+            nc.vector.tensor_tensor(
+                out=rb[c][:, cols].rearrange("p (r t) -> p r t", t=4),
+                in0=kb[:, cols].rearrange("p (r t) -> p r t", t=4),
+                in1=m1bank[c, b][:].rearrange("p (t r) -> p r t", t=4),
+                op=ALU.subtract)
 
         def qr(c):
             w = CHUNKS[c]
@@ -168,65 +199,109 @@ def tile_dictionarykvcachelistastep_x1_kernel(tc, k, z, a, dic, we, theta, out_0
             rs[c] = work.tile([P, 512], U8, name="rs", align_bytes=64)
             quant(rc[c][:, :w], rs[c][:, :w], rb[c][:, :4 * w])
 
-        def mm2(c, g):
+        def mm2(c, g, j):
             w = CHUNKS[c]
             per = BANK // w
-            for t in range(4):
-                if t % per == 0:
-                    pb = bank()
+            pb = bank()
+            for t in range(j * per, (j + 1) * per):
                 m2bank[c, g, t] = pb[:, (t % per) * w:(t % per + 1) * w]
                 nc.tensor.matmul_mx(
                     out=m2bank[c, g, t],
                     lhsT=we_c[:, g, t * P:(t + 1) * P].bitcast(X4), lhsT_scale=we_s[:, g, t * P:(t + 1) * P],
                     rhs=rc[c][:, :w].bitcast(X4), rhs_scale=rs[c][:, :w], start=True, stop=True)
 
-        def shift(c, g):
+        def p1(c, g, t):
             w = CHUNKS[c]
-            wt[c, g] = work.tile([P, 4, 512], F32, name="wt")
-            at[c, g] = work.tile([P, 4, 512], F32, name="at")
-            for t in range(4):
-                zb = zt[c][:, g, t // 2, :w].bitcast(BF16).rearrange("p (r e) -> p r e", e=2)[:, :, t % 2]
+            if (c, g) not in wt:
+                wt[c, g] = work.tile([P, 4, 512], F32, name="wt")
+            zb = zt[c][:, g, t // 2, :w].bitcast(BF16).rearrange("p (r e) -> p r e", e=2)[:, :, t % 2]
+            if (c, g, t) in OFF:
+                nc.gpsimd.tensor_tensor(out=wt[c, g][:, t, :w], in0=w0[c, g, t][:, :w], in1=zb, op=ALU.add)
+            else:
                 nc.vector.scalar_tensor_tensor(out=wt[c, g][:, t, :w], in0=m2bank[c, g, t], scalar=th[:, g, t:t + 1],
                                                in1=zb, op0=ALU.add, op1=ALU.add)
+
+        def ev(c, g, t):
+            if (c, g, t) in OFF:
+                w = CHUNKS[c]
+                w0[c, g, t] = work.tile([P, 512], F32, name="w0")
+                nc.scalar.activation(out=w0[c, g, t][:, :w], in_=m2bank[c, g, t], func=ACT.Identity,
+                                     bias=th[:, g, t:t + 1])
+
+        def relu(c, g, t):
+            w = CHUNKS[c]
+            if (c, g) not in at:
+                at[c, g] = work.tile([P, 4, 512], F32, name="at")
+            if (c, g, t) in RELUG:
+                nc.gpsimd.tensor_scalar(out=at[c, g][:, t, :w], in0=wt[c, g][:, t, :w], scalar1=th2[:, g, t:t + 1],
+                                        scalar2=0.0, op0=ALU.add, op1=ALU.max)
+            else:
                 nc.scalar.activation(out=at[c, g][:, t, :w], in_=wt[c, g][:, t, :w], func=ACT.Relu,
                                      bias=th2[:, g, t:t + 1])
 
-        def combine(c, g):
-            w = CHUNKS[c]
-            ot[c, g] = work.tile([P, 4, 512], F32, name="ot")
-            nc.vector.scalar_tensor_tensor(out=ot[c, g][:, :, :w], in0=wt[c, g][:, :, :w], scalar=0.0,
-                                           in1=at[c, g][:, :, :w], op0=ALU.min, op1=ALU.add)
+        def p3(c, g, h):
+            if (c, g) not in ot:
+                ot[c, g] = work.tile([P, 2, 4, HALF], F32, name="ot")
+            w = CHUNKS[c] // 2
+            nc.vector.scalar_tensor_tensor(out=ot[c, g][:, h, :, :w], in0=wt[c, g][:, :, h * w:(h + 1) * w], scalar=0.0,
+                                           in1=at[c, g][:, :, h * w:(h + 1) * w], op0=ALU.min, op1=ALU.add)
 
-        def cast(c, g):
-            w = CHUNKS[c]
-            ob[c, g] = work.tile([P, 2048], BF16, name="ob", align_bytes=64)
-            dst = ob[c, g][:, :4 * w].rearrange("p (r t) -> p r t", t=4)
-            src = ot[c, g][:, :, :w].rearrange("p t r -> p r t")
-            if c == n - 1 and g == 1:
+        def cast(c, g, h):
+            w = CHUNKS[c] // 2
+            if (c, g) not in ob:
+                ob[c, g] = work.tile([P, 2048], BF16, name="ob", bufs=3, align_bytes=64)
+            dst = ob[c, g][:, 4 * w * h:4 * w * (h + 1)].rearrange("p (r t) -> p r t", t=4)
+            src = ot[c, g][:, h, :, :w].rearrange("p t r -> p r t")
+            eng = CAST.get((c, g, h), "g")
+            if eng == "v":
                 nc.vector.tensor_copy(out=dst, in_=src)
+            elif eng == "s":
+                nc.scalar.copy(out=dst, in_=src)
             else:
                 nc.gpsimd.tensor_scalar(out=dst, in0=src, scalar1=1.0, scalar2=0.0, op0=ALU.mult, op1=ALU.add)
 
         def qo(c, g):
             w = CHUNKS[c]
-            oc = work.tile([P, 512], U32, name="oc", align_bytes=64)
+            oc = work.tile([P, 512], U32, name="oc", bufs=3, align_bytes=64)
             plane = out_s[1][:, g, :] if c == n - 1 else out_s[0][:, g, starts[c]:starts[c] + w]
             quant(oc[:, :w], plane, ob[c, g][:, :4 * w])
             nc.sync.dma_start(out=out_1[g].rearrange("p m t -> p (m t)").bitcast(I32)[:, starts[c]:starts[c] + w],
                               in_=oc[:, :w].bitcast(I32))
 
-        def to_eo(c, g):
-            nb = CHUNKS[c] // P
-            res = work.tile([P, 4, 512], F32, name="res", bufs=3)
-            for b in range(nb):
-                pb = bank()
-                for t in range(4):
-                    nc.tensor.transpose(pb[:, t * P:(t + 1) * P], ot[c, g][:, t, b * P:(b + 1) * P], ident[:])
-                nc.scalar.copy(out=res[:, b, :].rearrange("p (m t) -> p m t", t=4),
-                               in_=pb[:].rearrange("p (t m) -> p m t", t=4))
-            nc.sync.dma_start(
-                out=out_0[starts[c]:starts[c] + CHUNKS[c], g * 512:(g + 1) * 512].rearrange("(b p) x -> p b x", p=P),
-                in_=res[:, :nb, :])
+        def to(c, g, b):
+            per = CHUNKS[c] // 2 // P
+            pb = bank()
+            obank[c, g, b] = pb
+            for t in range(4):
+                nc.tensor.transpose(pb[:, t * P:(t + 1) * P],
+                                    ot[c, g][:, b // per, t, (b % per) * P:(b % per + 1) * P], ident[:])
+
+        def eo(c, g, b):
+            if b % 2 == 0:
+                rest[c, g, b // 2] = work.tile([P, 2, 512], F32, name="res", bufs=5)
+            res = rest[c, g, b // 2]
+            copy = nc.vector.tensor_copy if (c, g, b) in EOV else nc.scalar.copy
+            copy(out=res[:, b % 2, :].rearrange("p (m t) -> p m t", t=4),
+                 in_=obank[c, g, b][:].rearrange("p (t m) -> p m t", t=4))
+            r0 = starts[c] + b * P
+            if c == n - 1:
+                nc.sync.dma_start(out=out_0[r0:r0 + P, g * 512:(g + 1) * 512], in_=res[:, b % 2, :])
+            elif b % 2 == 1:
+                nc.sync.dma_start(
+                    out=out_0[r0 - P:r0 + P, g * 512:(g + 1) * 512].rearrange("(b p) x -> p b x", p=P), in_=res[:])
+
+        def il(name, g, q):
+            raw = (dic_raw if name == "d" else we_raw)[g]
+            if (name, g) not in grp:
+                grp[name, g] = work.tile([P, 2048], BF16, name="grouped", bufs=3, align_bytes=64)
+            dst = grp[name, g][:].rearrange("p (t m j) -> p t m j", t=4, j=4)[:, 2 * q:2 * q + 2]
+            src = raw[:].rearrange("p j (m t) -> p t m j", t=4)[:, 2 * q:2 * q + 2]
+            copy = nc.vector.tensor_copy if IL[name, g, q] == "v" else nc.scalar.copy
+            copy(out=dst, in_=src)
+
+        def qw(name, g):
+            codes, scales = (dic_c, dic_s) if name == "d" else (we_c, we_s)
+            quant(codes[:, g, :], scales[:, g, :], grp[name, g][:])
 
         def store_scales(part, m0, m1):
             for q in range(4):
@@ -234,82 +309,11 @@ def tile_dictionarykvcachelistastep_x1_kernel(tc, k, z, a, dic, we, theta, out_0
                     out=out_2.bitcast(I32)[:, 4 * q:4 * q + 4, m0 // 4:m1 // 4].rearrange("g r m -> r g m"),
                     in_=out_s[part][:].bitcast(I32)[32 * q:32 * q + 4, :, :])
 
-        gd0 = interleave(dic_raw[0], nc.vector.tensor_copy)
-        gd1 = interleave(dic_raw[1], nc.scalar.copy)
-        tz(0, 0)
-        za_ez(0, 0)
-        quant(dic_c[:, 0, :], dic_s[:, 0, :], gd0[:])
-        for h in halves(0)[1:]:
-            tz(0, h)
-            za_ez(0, h)
-        quant(dic_c[:, 1, :], dic_s[:, 1, :], gd1[:])
-        qz(0)
-        tk_ek(0)
-        mm1(0)
-        gw0 = interleave(we_raw[0], nc.vector.tensor_copy)
-        gw1 = interleave(we_raw[1], nc.scalar.copy)
-        residual(0)
-        quant(we_c[:, 0, :], we_s[:, 0, :], gw0[:])
-        qr(0)
-        tk_ek(1)
-        mm2(0, 0)
-        quant(we_c[:, 1, :], we_s[:, 1, :], gw1[:])
+        def ss(part):
+            store_scales(part, 0 if part == 0 else early, early if part == 0 else S)
 
-        for i in range(n):
-            more = i + 1 < n
-            if more:
-                for h in halves(i + 1):
-                    tz(i + 1, h)
-            shift(i, 0)
-            if more:
-                for h in halves(i + 1):
-                    za_ez(i + 1, h)
-            if i > 0:
-                to_eo(i - 1, 1)
-            if more:
-                qz(i + 1)
-            if i > 0 and CHUNKS[min(i + 1, n - 1)] == 512:
-                qo(i - 1, 1)
-            mm2(i, 1)
-            if more:
-                mm1(i + 1)
-            combine(i, 0)
-            if i > 0 and CHUNKS[min(i + 1, n - 1)] != 512:
-                qo(i - 1, 1)
-            if not more:
-                store_scales(0, 0, early)
-            cast(i, 0)
-            shift(i, 1)
-            to_eo(i, 0)
-            if more:
-                residual(i + 1)
-            if more:
-                qo(i, 0)
-                qr(i + 1)
-            if i + 2 < n:
-                tk_ek(i + 2)
-            if more:
-                mm2(i + 1, 0)
-            if more:
-                combine(i, 1)
-                cast(i, 1)
-        c = n - 1
-        w = CHUNKS[c]
-        ot[c, 1] = work.tile([P, 4, 512], F32, name="ot")
-        res = work.tile([P, 4, 512], F32, name="res", bufs=3)
-        for b in range(w // P):
-            blk = slice(b * P, (b + 1) * P)
-            nc.vector.scalar_tensor_tensor(out=ot[c, 1][:, :, blk], in0=wt[c, 1][:, :, blk], scalar=0.0,
-                                           in1=at[c, 1][:, :, blk], op0=ALU.min, op1=ALU.add)
-        qo(c, 0)
-        for b in range(w // P):
-            blk = slice(b * P, (b + 1) * P)
-            pb = bank()
-            for t in range(4):
-                nc.tensor.transpose(pb[:, t * P:(t + 1) * P], ot[c, 1][:, t, blk], ident[:])
-            nc.scalar.copy(out=res[:, b, :].rearrange("p (m t) -> p m t", t=4),
-                           in_=pb[:].rearrange("p (t m) -> p m t", t=4))
-            nc.sync.dma_start(out=out_0[starts[c] + b * P:starts[c] + (b + 1) * P, 512:1024], in_=res[:, b, :])
-        cast(c, 1)
-        qo(c, 1)
-        store_scales(1, early, S)
+        steps = {"tz": tz, "za": za_, "ez": ez, "qz": qz, "tk": tk, "ek": ek, "mm1": mm1, "rs": res_, "qr": qr,
+                 "mm2": mm2, "p1": p1, "relu": relu, "p3": p3, "cast": cast, "qo": qo, "to": to, "eo": eo,
+                 "ev": ev, "evp": evp, "tr": tr, "il": il, "qw": qw, "ss": ss}
+        for step in ORDER:
+            steps[step[0]](*step[1:])

@@ -16,23 +16,19 @@ ALU = mybir.AluOpType
 ACT = mybir.ActivationFunctionType
 
 P = 128
+GROUP = 512
 BANK = 512
-HALF = 256
+BANKS = 8
+PIECE = 256
 CHUNKS = [256, 512, 512, 512, 256]
-ORDER = [('tz', 0, 0, 0), ('il', 'd', 1, 1), ('il', 'd', 0, 1), ('il', 'd', 1, 0), ('il', 'd', 0, 0), ('qw', 'd', 0), ('tz', 0, 0, 1), ('il', 'w', 0, 1), ('za', 0, 0, 0), ('tk', 0, 0), ('il', 'w', 0, 0), ('za', 0, 0, 1), ('qw', 'd', 1), ('qz', 0), ('mm1', 0, 0), ('ek', 0, 0), ('mm1', 0, 1), ('tk', 1, 1), ('il', 'w', 1, 0), ('tk', 1, 0), ('evp', 0, 0), ('tr', 0, 0), ('il', 'w', 1, 1), ('evp', 0, 1), ('tr', 0, 1), ('qw', 'w', 0), ('ez', 0, 0, 0), ('rs', 0, 0), ('rs', 0, 1), ('qr', 0), ('tz', 1, 0, 0), ('ez', 0, 0, 1), ('mm2', 0, 0, 1), ('qw', 'w', 1), ('ev', 0, 0, 2), ('za', 1, 0, 0), ('ev', 0, 0, 3), ('mm2', 0, 0, 0), ('p1', 0, 0, 3), ('ez', 1, 0, 0), ('ev', 0, 0, 1), ('ev', 0, 0, 0), ('ek', 1, 1), ('p1', 0, 0, 0), ('tz', 1, 0, 1), ('tz', 1, 1, 1), ('ez', 1, 1, 1), ('ek', 1, 0), ('tz', 1, 1, 0), ('p1', 0, 0, 1), ('mm2', 0, 1, 0), ('ev', 0, 1, 1), ('ev', 0, 1, 0), ('relu', 0, 0, 1), ('p1', 0, 0, 2), ('relu', 0, 0, 2), ('za', 1, 0, 1), ('za', 1, 1, 0), ('za', 1, 1, 1), ('qz', 1), ('relu', 0, 0, 0), ('mm2', 0, 1, 1), ('ez', 1, 1, 0), ('mm1', 1, 3), ('mm1', 1, 1), ('relu', 0, 0, 3), ('mm1', 1, 2), ('p1', 0, 1, 0), ('ez', 1, 0, 1), ('p1', 0, 1, 1), ('p3', 0, 0, 0), ('mm1', 1, 0), ('ev', 0, 1, 2), ('evp', 1, 2), ('p1', 0, 1, 2), ('p3', 0, 0, 1), ('evp', 1, 3), ('evp', 1, 0), ('tr', 1, 3), ('evp', 1, 1), ('tr', 1, 2), ('rs', 1, 3), ('relu', 0, 1, 1), ('relu', 0, 1, 2), ('tr', 1, 0), ('ev', 0, 1, 3), ('tr', 1, 1), ('to', 0, 0, 0), ('relu', 0, 1, 0), ('rs', 1, 1), ('eo', 0, 0, 0), ('cast', 0, 0, 1), ('rs', 1, 2), ('rs', 1, 0), ('p1', 0, 1, 3), ('relu', 0, 1, 3), ('to', 0, 0, 1), ('tk', 2, 1), ('eo', 0, 0, 1), ('cast', 0, 0, 0), ('qr', 1), ('qo', 0, 0), ('p3', 0, 1, 1), ('tk', 2, 0), ('mm2', 1, 0, 2), ('mm2', 1, 0, 1), ('p3', 0, 1, 0), ('ek', 2, 1), ('mm2', 1, 0, 0), ('cast', 0, 1, 1), ('mm2', 1, 0, 3), ('ek', 2, 0), ('cast', 0, 1, 0), ('ev', 1, 0, 0), ('ev', 1, 0, 1), ('p1', 1, 0, 1), ('ev', 1, 0, 2), ('tz', 2, 0, 0), ('tz', 2, 1, 0), ('p1', 1, 0, 2), ('tz', 2, 0, 1), ('p1', 1, 0, 0), ('za', 2, 0, 0), ('ez', 2, 1, 0), ('ev', 1, 0, 3), ('tz', 2, 1, 1), ('relu', 1, 0, 0), ('mm2', 1, 1, 2), ('relu', 1, 0, 2), ('p1', 1, 0, 3), ('za', 2, 0, 1), ('ev', 1, 1, 2), ('mm2', 1, 1, 0), ('za', 2, 1, 0), ('mm2', 1, 1, 1), ('ez', 2, 0, 0), ('relu', 1, 0, 3), ('ez', 2, 0, 1), ('ev', 1, 1, 0), ('za', 2, 1, 1), ('qz', 2), ('qo', 0, 1), ('to', 0, 1, 0), ('relu', 1, 0, 1), ('mm2', 1, 1, 3), ('mm1', 2, 0), ('to', 0, 1, 1), ('ev', 1, 1, 1), ('ev', 1, 1, 3), ('p3', 1, 0, 0), ('p3', 1, 0, 1), ('eo', 0, 1, 0), ('evp', 2, 0), ('p1', 1, 1, 2), ('ez', 2, 1, 1), ('p1', 1, 1, 0), ('mm1', 2, 1), ('mm1', 2, 2), ('mm1', 2, 3), ('p1', 1, 1, 1), ('evp', 2, 2), ('evp', 2, 3), ('cast', 1, 0, 1), ('evp', 2, 1), ('cast', 1, 0, 0), ('eo', 0, 1, 1), ('to', 1, 0, 0), ('p1', 1, 1, 3), ('tr', 2, 0), ('tr', 2, 1), ('tr', 2, 2), ('to', 1, 0, 2), ('rs', 2, 0), ('relu', 1, 1, 2), ('relu', 1, 1, 1), ('rs', 2, 1), ('relu', 1, 1, 3), ('tk', 3, 1), ('rs', 2, 2), ('relu', 1, 1, 0), ('eo', 1, 0, 0), ('tk', 3, 0), ('to', 1, 0, 1), ('eo', 1, 0, 2), ('tr', 2, 3), ('rs', 2, 3), ('qo', 1, 0), ('qr', 2), ('to', 1, 0, 3), ('mm2', 2, 0, 2), ('ek', 3, 1), ('p3', 1, 1, 1), ('p3', 1, 1, 0), ('ek', 3, 0), ('mm2', 2, 0, 1), ('mm2', 2, 0, 0), ('eo', 1, 0, 1), ('eo', 1, 0, 3), ('cast', 1, 1, 1), ('cast', 1, 1, 0), ('mm2', 2, 0, 3), ('to', 1, 1, 2), ('ev', 2, 0, 0), ('ev', 2, 0, 1), ('p1', 2, 0, 1), ('ev', 2, 0, 2), ('tz', 3, 0, 0), ('tz', 3, 1, 0), ('p1', 2, 0, 2), ('tz', 3, 0, 1), ('p1', 2, 0, 0), ('to', 1, 1, 3), ('eo', 1, 1, 2), ('za', 3, 0, 0), ('ez', 3, 1, 0), ('ev', 2, 0, 3), ('tz', 3, 1, 1), ('relu', 2, 0, 0), ('mm2', 2, 1, 2), ('relu', 2, 0, 2), ('p1', 2, 0, 3), ('za', 3, 0, 1), ('ev', 2, 1, 2), ('mm2', 2, 1, 0), ('za', 3, 1, 0), ('mm2', 2, 1, 1), ('ez', 3, 0, 0), ('relu', 2, 0, 3), ('eo', 1, 1, 3), ('ez', 3, 0, 1), ('ev', 2, 1, 0), ('za', 3, 1, 1), ('qz', 3), ('qo', 1, 1), ('to', 1, 1, 0), ('relu', 2, 0, 1), ('mm2', 2, 1, 3), ('mm1', 3, 0), ('to', 1, 1, 1), ('ev', 2, 1, 1), ('ev', 2, 1, 3), ('p3', 2, 0, 0), ('p3', 2, 0, 1), ('eo', 1, 1, 0), ('evp', 3, 0), ('p1', 2, 1, 2), ('ez', 3, 1, 1), ('p1', 2, 1, 0), ('mm1', 3, 1), ('mm1', 3, 2), ('mm1', 3, 3), ('p1', 2, 1, 1), ('evp', 3, 2), ('evp', 3, 3), ('cast', 2, 0, 1), ('evp', 3, 1), ('cast', 2, 0, 0), ('eo', 1, 1, 1), ('to', 2, 0, 0), ('p1', 2, 1, 3), ('tr', 3, 0), ('tr', 3, 1), ('tr', 3, 2), ('to', 2, 0, 2), ('rs', 3, 0), ('relu', 2, 1, 2), ('relu', 2, 1, 1), ('rs', 3, 1), ('relu', 2, 1, 3), ('rs', 3, 2), ('relu', 2, 1, 0), ('eo', 2, 0, 0), ('tk', 4, 0), ('to', 2, 0, 1), ('eo', 2, 0, 2), ('tr', 3, 3), ('rs', 3, 3), ('qo', 2, 0), ('qr', 3), ('to', 2, 0, 3), ('mm2', 3, 0, 2), ('p3', 2, 1, 1), ('p3', 2, 1, 0), ('ek', 4, 0), ('mm2', 3, 0, 1), ('mm2', 3, 0, 0), ('eo', 2, 0, 1), ('eo', 2, 0, 3), ('cast', 2, 1, 1), ('cast', 2, 1, 0), ('mm2', 3, 0, 3), ('to', 2, 1, 2), ('ev', 3, 0, 0), ('ev', 3, 0, 1), ('p1', 3, 0, 1), ('ev', 3, 0, 2), ('tz', 4, 0, 0), ('p1', 3, 0, 2), ('tz', 4, 0, 1), ('p1', 3, 0, 0), ('to', 2, 1, 3), ('eo', 2, 1, 2), ('za', 4, 0, 0), ('ev', 3, 0, 3), ('relu', 3, 0, 0), ('mm2', 3, 1, 2), ('relu', 3, 0, 2), ('p1', 3, 0, 3), ('za', 4, 0, 1), ('ev', 3, 1, 2), ('mm2', 3, 1, 0), ('mm2', 3, 1, 1), ('ez', 4, 0, 0), ('relu', 3, 0, 3), ('eo', 2, 1, 3), ('ez', 4, 0, 1), ('ev', 3, 1, 0), ('qz', 4), ('qo', 2, 1), ('to', 2, 1, 0), ('relu', 3, 0, 1), ('mm2', 3, 1, 3), ('mm1', 4, 0), ('to', 2, 1, 1), ('ev', 3, 1, 1), ('ev', 3, 1, 3), ('p3', 3, 0, 0), ('p3', 3, 0, 1), ('eo', 2, 1, 0), ('evp', 4, 0), ('p1', 3, 1, 2), ('p1', 3, 1, 0), ('mm1', 4, 1), ('p1', 3, 1, 1), ('cast', 3, 0, 1), ('evp', 4, 1), ('cast', 3, 0, 0), ('eo', 2, 1, 1), ('to', 3, 0, 0), ('p1', 3, 1, 3), ('tr', 4, 0), ('tr', 4, 1), ('to', 3, 0, 2), ('rs', 4, 0), ('relu', 3, 1, 2), ('relu', 3, 1, 1), ('rs', 4, 1), ('relu', 3, 1, 3), ('relu', 3, 1, 0), ('eo', 3, 0, 0), ('to', 3, 0, 1), ('eo', 3, 0, 2), ('qo', 3, 0), ('qr', 4), ('to', 3, 0, 3), ('p3', 3, 1, 1), ('p3', 3, 1, 0), ('mm2', 4, 0, 1), ('mm2', 4, 0, 0), ('eo', 3, 0, 1), ('eo', 3, 0, 3), ('cast', 3, 1, 1), ('cast', 3, 1, 0), ('ev', 4, 0, 3), ('mm2', 4, 1, 0), ('mm2', 4, 1, 1), ('to', 3, 1, 0), ('ev', 4, 0, 1), ('ev', 4, 1, 0), ('p1', 4, 0, 1), ('ev', 4, 0, 0), ('p1', 4, 0, 3), ('ev', 4, 1, 2), ('relu', 4, 0, 1), ('to', 3, 1, 3), ('p1', 4, 0, 0), ('p1', 4, 1, 2), ('ev', 4, 0, 2), ('relu', 4, 0, 3), ('eo', 3, 1, 0), ('to', 3, 1, 1), ('ev', 4, 1, 3), ('to', 3, 1, 2), ('p1', 4, 1, 0), ('p1', 4, 0, 2), ('relu', 4, 0, 0), ('ev', 4, 1, 1), ('relu', 4, 1, 2), ('p1', 4, 1, 1), ('relu', 4, 0, 2), ('eo', 3, 1, 2), ('p1', 4, 1, 3), ('eo', 3, 1, 1), ('eo', 3, 1, 3), ('p3', 4, 0, 0), ('p3', 4, 0, 1), ('qo', 3, 1), ('ss', 0), ('relu', 4, 1, 3), ('to', 4, 0, 0), ('relu', 4, 1, 1), ('to', 4, 0, 1), ('relu', 4, 1, 0), ('eo', 4, 0, 0), ('p3', 4, 1, 0), ('eo', 4, 0, 1), ('p3', 4, 1, 1), ('to', 4, 1, 0), ('cast', 4, 1, 1), ('cast', 4, 0, 0), ('to', 4, 1, 1), ('eo', 4, 1, 0), ('eo', 4, 1, 1), ('cast', 4, 1, 0), ('cast', 4, 0, 1), ('qo', 4, 0), ('qo', 4, 1), ('ss', 1)]
-LOADS = [('d', 0), ('d', 1), ('z', 0), ('k', 0), ('w', 0), ('k', 2), ('k', 3), ('w', 1), ('k', 1), ('z', 1), ('z', 2), ('z', 3), ('z', 4), ('k', 4), ('z', 5), ('k', 5), ('z', 6), ('k', 6), ('z', 7), ('k', 7)]
-CAST = {(0, 0, 0): 'g', (0, 0, 1): 'g', (0, 1, 0): 'g', (0, 1, 1): 'g', (1, 0, 0): 's', (1, 0, 1): 'g', (1, 1, 0): 's', (1, 1, 1): 'g', (2, 0, 0): 's', (2, 0, 1): 'g', (2, 1, 0): 's', (2, 1, 1): 'g', (3, 0, 0): 's', (3, 0, 1): 'g', (3, 1, 0): 'g', (3, 1, 1): 's', (4, 0, 0): 'g', (4, 0, 1): 's', (4, 1, 0): 'v', (4, 1, 1): 's'}
-EOV = {(3, 1, 3), (4, 1, 0), (4, 1, 1), (3, 1, 1)}
-OFF = {(2, 1, 0), (3, 1, 0), (1, 1, 0)}
-RELUG = {(1, 0, 1), (2, 0, 2), (2, 0, 1), (3, 0, 2), (3, 0, 1), (1, 0, 2)}
-RPE = set()
-IL = {('d', 0, 0): 'v', ('d', 0, 1): 'v', ('d', 1, 0): 'v', ('d', 1, 1): 's', ('w', 0, 0): 's', ('w', 0, 1): 's', ('w', 1, 0): 'v', ('w', 1, 1): 's'}
+WIDEST = max(CHUNKS)
+LAST = len(CHUNKS) - 1
+STARTS = [sum(CHUNKS[:c]) for c in range(len(CHUNKS))]
+WARM_UP = (4, 5)
 
 
 def tile_dictionarykvcachelistastep_x1_kernel(tc, k, z, a, dic, we, theta, out_0, out_1, out_2):
     nc = tc.nc
-    n = len(CHUNKS)
-    starts = [sum(CHUNKS[:c]) for c in range(n)]
 
     with ExitStack() as ctx:
         keep = ctx.enter_context(tc.tile_pool(name="keep", bufs=1))
@@ -40,280 +36,337 @@ def tile_dictionarykvcachelistastep_x1_kernel(tc, k, z, a, dic, we, theta, out_0
         psum = ctx.enter_context(tc.psum_pool(name="psum", bufs=1))
         ctx.enter_context(tc.manual_schedule())
 
-        used = []
+        taken = []
 
         def bank():
-            used.append(len(used) % 8)
-            return psum.tile([P, BANK], F32, name="bank%d" % used[-1])
+            taken.append(len(taken) % BANKS)
+            return psum.tile([P, BANK], F32, name="bank%d" % taken[-1])
 
         ident = keep.tile([P, P], F32, name="ident")
         make_identity(nc, ident[:])
-        ident_b = keep.tile([P, P], BF16, name="ident_b")
-        make_identity(nc, ident_b[:])
 
-        a_t = keep.tile([P, 2, 4], BF16, name="a_t")
-        th = keep.tile([P, 2, 4], BF16, name="th")
-        th2 = keep.tile([P, 2, 4], F32, name="th2")
-        nc.scalar.dma_start(out=a_t[:], in_=a.rearrange("(g p t) -> p g t", g=2, t=4))
-        nc.scalar.dma_start(out=th[:], in_=theta.rearrange("(g p t) -> p g t", g=2, t=4))
+        a_sb = keep.tile([P, 2, 4], BF16, name="a_sb")
+        theta_sb = keep.tile([P, 2, 4], BF16, name="theta_sb")
+        minus_2theta = keep.tile([P, 2, 4], F32, name="minus_2theta")
+        nc.scalar.dma_start(out=a_sb[:], in_=a.rearrange("(g p t) -> p g t", g=2, t=4))
+        nc.scalar.dma_start(out=theta_sb[:], in_=theta.rearrange("(g p t) -> p g t", g=2, t=4))
 
-        z_sb = [keep.tile([P, 2, A], BF16, name="z%d" % h) for h in range(S // HALF)]
-        k_sb = [keep.tile([P, 2, DK], BF16, name="k%d" % h) for h in range(S // HALF)]
-        dic_raw = [keep.tile([P, 4, DK], BF16, name="dicraw%d" % g) for g in range(2)]
-        we_raw = [keep.tile([P, 4, 512], BF16, name="weraw%d" % g) for g in range(2)]
+        z_sb = [keep.tile([P, 2, A], BF16, name="z%d" % j) for j in range(S // PIECE)]
+        k_sb = [keep.tile([P, 2, DK], BF16, name="k%d" % j) for j in range(S // PIECE)]
+        dic_raw = [keep.tile([P, 4, DK], BF16, name="dic_raw%d" % g) for g in range(2)]
+        we_raw = [keep.tile([P, 4, GROUP], BF16, name="we_raw%d" % g) for g in range(2)]
 
-        def load_z(h):
-            nc.sync.dma_start(out=z_sb[h][:], in_=z[h * HALF:(h + 1) * HALF, :].rearrange("(b p) x -> p b x", p=P))
+        def load_tokens(tiles, src, j):
+            nc.sync.dma_start(out=tiles[j][:], in_=src[j * PIECE:(j + 1) * PIECE, :].rearrange("(b p) x -> p b x", p=P))
 
-        def load_k(h):
-            nc.sync.dma_start(out=k_sb[h][:], in_=k[h * HALF:(h + 1) * HALF, :].rearrange("(b p) x -> p b x", p=P))
+        def load_weight(tile, src):
+            nc.sync.dma_start(out=tile[:], in_=src.rearrange("(p j) x -> p j x", j=4))
 
-        def load_dic(g):
-            nc.sync.dma_start(out=dic_raw[g][:], in_=dic[g * 512:(g + 1) * 512, :].rearrange("(p j) x -> p j x", j=4))
+        load_tokens(z_sb, z, 0)
+        load_weight(dic_raw[0], dic[0:GROUP, :])
+        load_weight(dic_raw[1], dic[GROUP:A, :])
+        load_tokens(k_sb, k, 0)
+        load_weight(we_raw[0], we[:, 0:GROUP])
+        load_tokens(z_sb, z, 1)
+        load_weight(we_raw[1], we[:, GROUP:A])
+        load_tokens(z_sb, z, 2)
+        load_tokens(k_sb, k, 1)
+        load_tokens(k_sb, k, 2)
+        for j in range(3, S // PIECE):
+            load_tokens(z_sb, z, j)
+            load_tokens(k_sb, k, j)
 
-        def load_we(g):
-            nc.sync.dma_start(out=we_raw[g][:], in_=we[:, g * 512:(g + 1) * 512].rearrange("(p j) x -> p j x", j=4))
+        nc.scalar.mul(out=minus_2theta[:], in_=theta_sb[:], mul=-2.0)
 
-        loads = {"d": load_dic, "z": load_z, "k": load_k, "w": load_we}
-        for name, j in LOADS:
-            loads[name](j)
+        dic_codes = keep.tile([P, 2, DK], U32, name="dic_codes", align_bytes=64)
+        dic_scales = keep.tile([P, 2, DK], U8, name="dic_scales", align_bytes=64)
+        we_codes = keep.tile([P, 2, GROUP], U32, name="we_codes", align_bytes=64)
+        we_scales = keep.tile([P, 2, GROUP], U8, name="we_scales", align_bytes=64)
+        early_scales = keep.tile([P, 2, STARTS[LAST]], U8, name="early_scales", align_bytes=64)
+        last_scales = keep.tile([P, 2, CHUNKS[LAST]], U8, name="last_scales", align_bytes=64)
 
-        nc.scalar.mul(out=th2[:], in_=th[:], mul=-2.0)
+        z_banks, z_words, za, za_codes, za_scales = {}, {}, {}, {}, {}
+        k_words, recon_banks, r_codes, r_scales, resid = {}, {}, {}, {}, {}
+        enc_banks, shifted, upper, result, rounded, back_banks, rows = {}, {}, {}, {}, {}, {}, {}
 
-        dic_c = keep.tile([P, 2, 512], U32, name="dic_c", align_bytes=64)
-        dic_s = keep.tile([P, 2, 512], U8, name="dic_s", align_bytes=64)
-        we_c = keep.tile([P, 2, 512], U32, name="we_c", align_bytes=64)
-        we_s = keep.tile([P, 2, 512], U8, name="we_s", align_bytes=64)
-        early = starts[n - 1]
-        out_s = [keep.tile([P, 2, early], U8, name="out_s0", align_bytes=64),
-                 keep.tile([P, 2, S - early], U8, name="out_s1", align_bytes=64)]
+        def pieces(c):
+            return range(CHUNKS[c] // PIECE)
 
-        def quant(codes, scales, src):
+        def blocks(c):
+            return range(CHUNKS[c] // P)
+
+        def quantise(codes, scales, src):
             nc.vector.quantize_mx(out=codes.bitcast(X4), scales=scales, in_=src)
 
-        zt, kt, za, zc, zs, rb, rc, rs = {}, {}, {}, {}, {}, {}, {}, {}
-        kbank, obank, rest, grp, w0, neg, rbank = {}, {}, {}, {}, {}, {}, {}
-        zbank, m1bank, m2bank, wt, at, ot, ob = {}, {}, {}, {}, {}, {}, {}
+        def lay_out_weight(raw, first, second):
+            laid = work.tile([P, 4 * GROUP], BF16, name="laid", bufs=3, align_bytes=64)
+            dst = laid[:].rearrange("p (t m j) -> p t m j", t=4, j=4)
+            src = raw[:].rearrange("p j (m t) -> p t m j", t=4)
+            first(out=dst[:, 0:2], in_=src[:, 0:2])
+            second(out=dst[:, 2:4], in_=src[:, 2:4])
+            return laid
 
-        def halves(c):
-            return range(CHUNKS[c] // HALF)
+        def warm_up(count):
+            unread = bank()
+            for j in range(count):
+                nc.tensor.matmul(unread[:], lhsT=z_sb[0][:, 0, 0:P], rhs=z_sb[0][:, 0, 0:BANK], start=True, stop=True)
 
-        def transpose_words(src, col0):
-            pb = bank()
+        def transpose_words(src, word0):
+            turned = bank()
             words = src[:].bitcast(F32)
             for b in range(2):
                 for u in range(2):
-                    nc.tensor.transpose(pb[:, u * HALF + b * P:u * HALF + (b + 1) * P],
-                                        words[:, b, col0 + u:col0 + 256:2], ident[:])
-            return pb
+                    nc.tensor.transpose(turned[:, u * PIECE + b * P:u * PIECE + (b + 1) * P],
+                                        words[:, b, word0 + u:word0 + GROUP // 2:2], ident[:])
+            return turned
 
-        def tz(c, h, g):
-            zbank[c, h, g] = transpose_words(z_sb[starts[c] // HALF + h], 256 * g)
+        def turn_z(c, h):
+            for g in range(2):
+                z_banks[c, h, g] = transpose_words(z_sb[STARTS[c] // PIECE + h], g * GROUP // 2)
 
-        def za_(c, h, g):
+        def scale_z(c, h, g):
             if c not in za:
-                za[c] = work.tile([P, 2, 2048], BF16, name="za", bufs=1, align_bytes=64)
+                za[c] = work.tile([P, 2, 4 * WIDEST], BF16, name="za", bufs=1, align_bytes=64)
             nc.vector.tensor_tensor(
-                out=za[c][:, g, h * 4 * HALF:(h + 1) * 4 * HALF].rearrange("p (r u e) -> p r u e", u=2, e=2),
-                in0=zbank[c, h, g][:].bitcast(BF16).rearrange("p (u r e) -> p r u e", u=2, e=2),
-                in1=a_t[:, g:g + 1, :].rearrange("p o (u e) -> p o u e", u=2).to_broadcast([P, HALF, 2, 2]),
+                out=za[c][:, g, h * 4 * PIECE:(h + 1) * 4 * PIECE].rearrange("p (r u e) -> p r u e", u=2, e=2),
+                in0=z_banks[c, h, g][:].bitcast(BF16).rearrange("p (u r e) -> p r u e", u=2, e=2),
+                in1=a_sb[:, g:g + 1, :].rearrange("p o (u e) -> p o u e", u=2).to_broadcast([P, PIECE, 2, 2]),
                 op=ALU.mult)
 
-        def ez(c, h, g):
-            if c not in zt:
-                zt[c] = work.tile([P, 2, 2, 512], F32, name="zt")
-            nc.scalar.copy(out=zt[c][:, g, :, h * HALF:(h + 1) * HALF],
-                           in_=zbank[c, h, g][:].rearrange("p (u r) -> p u r", u=2))
+        def keep_z(c, h, g):
+            if c not in z_words:
+                z_words[c] = work.tile([P, 2, 2, WIDEST], F32, name="z_words")
+            nc.scalar.copy(out=z_words[c][:, g, :, h * PIECE:(h + 1) * PIECE],
+                           in_=z_banks[c, h, g][:].rearrange("p (u r) -> p u r", u=2))
 
-        def qz(c):
-            w = CHUNKS[c]
-            zc[c] = work.tile([P, 2, 512], U32, name="zc", align_bytes=64)
-            zs[c] = work.tile([P, 2, 512], U8, name="zs", align_bytes=64)
+        def scale_and_keep_z(c, h):
             for g in range(2):
-                quant(zc[c][:, g, :w], zs[c][:, g, :w], za[c][:, g, :4 * w])
+                scale_z(c, h, g)
+                keep_z(c, h, g)
 
-        def tk(c, h):
-            if (c, h) in RPE:
-                return
-            kbank[c, h] = transpose_words(k_sb[starts[c] // HALF + h], 0)
+        def quantise_za(c):
+            w = CHUNKS[c]
+            za_codes[c] = work.tile([P, 2, WIDEST], U32, name="za_codes", align_bytes=64)
+            za_scales[c] = work.tile([P, 2, WIDEST], U8, name="za_scales", align_bytes=64)
+            for g in range(2):
+                quantise(za_codes[c][:, g, :w], za_scales[c][:, g, :w], za[c][:, g, :4 * w])
 
-        def ek(c, h):
-            if (c, h) in RPE:
-                return
-            if c not in kt:
-                kt[c] = work.tile([P, 512, 2], F32, name="kt")
-            nc.scalar.copy(out=kt[c][:, h * HALF:(h + 1) * HALF, :], in_=kbank[c, h][:].rearrange("p (u r) -> p r u", u=2))
+        def turn_k(c):
+            turned = [transpose_words(k_sb[STARTS[c] // PIECE + h], 0) for h in pieces(c)]
+            k_words[c] = work.tile([P, WIDEST, 2], F32, name="k_words")
+            for h in pieces(c):
+                nc.scalar.copy(out=k_words[c][:, h * PIECE:(h + 1) * PIECE, :],
+                               in_=turned[h][:].rearrange("p (u r) -> p r u", u=2))
 
-        def mm1(c, b):
-            pb = bank()
-            m1bank[c, b] = pb
-            if (c, b // 2) in RPE:
-                for g in range(2):
-                    nc.tensor.matmul_mx(
-                        out=pb[:], lhsT=zc[c][:, g, b * P:(b + 1) * P].bitcast(X4),
-                        lhsT_scale=zs[c][:, g, b * P:(b + 1) * P],
-                        rhs=dic_c[:, g, :].bitcast(X4), rhs_scale=dic_s[:, g, :], start=(g == 0), stop=(g == 1))
-                return
-            for t in range(4):
-                for g in range(2):
-                    nc.tensor.matmul_mx(
-                        out=pb[:, t * P:(t + 1) * P],
-                        lhsT=dic_c[:, g, t * P:(t + 1) * P].bitcast(X4), lhsT_scale=dic_s[:, g, t * P:(t + 1) * P],
-                        rhs=zc[c][:, g, b * P:(b + 1) * P].bitcast(X4), rhs_scale=zs[c][:, g, b * P:(b + 1) * P],
-                        start=(g == 0), stop=(g == 1))
-
-        def evp(c, b):
-            if (c, b // 2) in RPE:
-                neg[c, b] = work.tile([P, 512], F32, name="neg")
-                nc.scalar.mul(out=neg[c, b][:], in_=m1bank[c, b][:], mul=-1.0)
-
-        def tr(c, b):
-            if (c, b // 2) in RPE:
-                pb = bank()
-                rbank[c, b] = pb
-                rows = k_sb[starts[c] // HALF + b // 2]
+        def reconstruct(c):
+            for b in blocks(c):
+                recon_banks[c, b] = bank()
+                tokens = slice(b * P, (b + 1) * P)
                 for t in range(4):
-                    nc.tensor.matmul(pb[:, t * P:(t + 1) * P], lhsT=rows[:, b % 2, t:DK:4], rhs=ident_b[:],
-                                     start=True, stop=False)
-                    nc.tensor.matmul(pb[:, t * P:(t + 1) * P], lhsT=neg[c, b][:, t * P:(t + 1) * P], rhs=ident[:],
-                                     start=False, stop=True, is_transpose=True)
+                    cols = slice(t * P, (t + 1) * P)
+                    for g in range(2):
+                        nc.tensor.matmul_mx(
+                            out=recon_banks[c, b][:, cols],
+                            lhsT=dic_codes[:, g, cols].bitcast(X4), lhsT_scale=dic_scales[:, g, cols],
+                            rhs=za_codes[c][:, g, tokens].bitcast(X4), rhs_scale=za_scales[c][:, g, tokens],
+                            start=(g == 0), stop=(g == 1))
 
-        def res_(c, b):
-            if c not in rb:
-                rb[c] = work.tile([P, 2048], BF16, name="rb", bufs=1, align_bytes=64)
-            if (c, b // 2) in RPE:
-                nc.scalar.copy(out=rb[c][:, b * 512:(b + 1) * 512].rearrange("p (r t) -> p r t", t=4),
-                               in_=rbank[c, b][:].rearrange("p (t r) -> p r t", t=4))
-                return
-            kb = kt[c][:].rearrange("p r u -> p (r u)").bitcast(BF16)
-            cols = slice(b * 512, (b + 1) * 512)
-            nc.vector.tensor_tensor(
-                out=rb[c][:, cols].rearrange("p (r t) -> p r t", t=4),
-                in0=kb[:, cols].rearrange("p (r t) -> p r t", t=4),
-                in1=m1bank[c, b][:].rearrange("p (t r) -> p r t", t=4),
-                op=ALU.subtract)
+        def subtract_from_k(c):
+            resid[c] = work.tile([P, 4 * WIDEST], BF16, name="resid", bufs=1, align_bytes=64)
+            k_turned = k_words[c][:].rearrange("p r u -> p (r u)").bitcast(BF16)
+            for b in blocks(c):
+                cols = slice(b * 4 * P, (b + 1) * 4 * P)
+                nc.vector.tensor_tensor(
+                    out=resid[c][:, cols].rearrange("p (r t) -> p r t", t=4),
+                    in0=k_turned[:, cols].rearrange("p (r t) -> p r t", t=4),
+                    in1=recon_banks[c, b][:].rearrange("p (t r) -> p r t", t=4),
+                    op=ALU.subtract)
 
-        def qr(c):
+        def quantise_resid(c):
             w = CHUNKS[c]
-            rc[c] = work.tile([P, 512], U32, name="rc", align_bytes=64)
-            rs[c] = work.tile([P, 512], U8, name="rs", align_bytes=64)
-            quant(rc[c][:, :w], rs[c][:, :w], rb[c][:, :4 * w])
+            r_codes[c] = work.tile([P, WIDEST], U32, name="r_codes", align_bytes=64)
+            r_scales[c] = work.tile([P, WIDEST], U8, name="r_scales", align_bytes=64)
+            quantise(r_codes[c][:, :w], r_scales[c][:, :w], resid[c][:, :4 * w])
 
-        def mm2(c, g, j):
+        def encode(c, g):
             w = CHUNKS[c]
-            per = BANK // w
-            pb = bank()
-            for t in range(j * per, (j + 1) * per):
-                m2bank[c, g, t] = pb[:, (t % per) * w:(t % per + 1) * w]
-                nc.tensor.matmul_mx(
-                    out=m2bank[c, g, t],
-                    lhsT=we_c[:, g, t * P:(t + 1) * P].bitcast(X4), lhsT_scale=we_s[:, g, t * P:(t + 1) * P],
-                    rhs=rc[c][:, :w].bitcast(X4), rhs_scale=rs[c][:, :w], start=True, stop=True)
-
-        def p1(c, g, t):
-            w = CHUNKS[c]
-            if (c, g) not in wt:
-                wt[c, g] = work.tile([P, 4, 512], F32, name="wt")
-            zb = zt[c][:, g, t // 2, :w].bitcast(BF16).rearrange("p (r e) -> p r e", e=2)[:, :, t % 2]
-            if (c, g, t) in OFF:
-                nc.gpsimd.tensor_tensor(out=wt[c, g][:, t, :w], in0=w0[c, g, t][:, :w], in1=zb, op=ALU.add)
-            else:
-                nc.vector.scalar_tensor_tensor(out=wt[c, g][:, t, :w], in0=m2bank[c, g, t], scalar=th[:, g, t:t + 1],
-                                               in1=zb, op0=ALU.add, op1=ALU.add)
-
-        def ev(c, g, t):
-            if (c, g, t) in OFF:
-                w = CHUNKS[c]
-                w0[c, g, t] = work.tile([P, 512], F32, name="w0")
-                nc.scalar.activation(out=w0[c, g, t][:, :w], in_=m2bank[c, g, t], func=ACT.Identity,
-                                     bias=th[:, g, t:t + 1])
-
-        def relu(c, g, t):
-            w = CHUNKS[c]
-            if (c, g) not in at:
-                at[c, g] = work.tile([P, 4, 512], F32, name="at")
-            if (c, g, t) in RELUG:
-                nc.gpsimd.tensor_scalar(out=at[c, g][:, t, :w], in0=wt[c, g][:, t, :w], scalar1=th2[:, g, t:t + 1],
-                                        scalar2=0.0, op0=ALU.add, op1=ALU.max)
-            else:
-                nc.scalar.activation(out=at[c, g][:, t, :w], in_=wt[c, g][:, t, :w], func=ACT.Relu,
-                                     bias=th2[:, g, t:t + 1])
-
-        def p3(c, g, h):
-            if (c, g) not in ot:
-                ot[c, g] = work.tile([P, 2, 4, HALF], F32, name="ot")
-            w = CHUNKS[c] // 2
-            nc.vector.scalar_tensor_tensor(out=ot[c, g][:, h, :, :w], in0=wt[c, g][:, :, h * w:(h + 1) * w], scalar=0.0,
-                                           in1=at[c, g][:, :, h * w:(h + 1) * w], op0=ALU.min, op1=ALU.add)
-
-        def cast(c, g, h):
-            w = CHUNKS[c] // 2
-            if (c, g) not in ob:
-                ob[c, g] = work.tile([P, 2048], BF16, name="ob", bufs=3, align_bytes=64)
-            dst = ob[c, g][:, 4 * w * h:4 * w * (h + 1)].rearrange("p (r t) -> p r t", t=4)
-            src = ot[c, g][:, h, :, :w].rearrange("p t r -> p r t")
-            eng = CAST.get((c, g, h), "g")
-            if eng == "v":
-                nc.vector.tensor_copy(out=dst, in_=src)
-            elif eng == "s":
-                nc.scalar.copy(out=dst, in_=src)
-            else:
-                nc.gpsimd.tensor_scalar(out=dst, in0=src, scalar1=1.0, scalar2=0.0, op0=ALU.mult, op1=ALU.add)
-
-        def qo(c, g):
-            w = CHUNKS[c]
-            oc = work.tile([P, 512], U32, name="oc", bufs=3, align_bytes=64)
-            plane = out_s[1][:, g, :] if c == n - 1 else out_s[0][:, g, starts[c]:starts[c] + w]
-            quant(oc[:, :w], plane, ob[c, g][:, :4 * w])
-            nc.sync.dma_start(out=out_1[g].rearrange("p m t -> p (m t)").bitcast(I32)[:, starts[c]:starts[c] + w],
-                              in_=oc[:, :w].bitcast(I32))
-
-        def to(c, g, b):
-            per = CHUNKS[c] // 2 // P
-            pb = bank()
-            obank[c, g, b] = pb
+            per_bank = BANK // w
             for t in range(4):
-                nc.tensor.transpose(pb[:, t * P:(t + 1) * P],
-                                    ot[c, g][:, b // per, t, (b % per) * P:(b % per + 1) * P], ident[:])
+                if t % per_bank == 0:
+                    enc = bank()
+                enc_banks[c, g, t] = enc[:, (t % per_bank) * w:(t % per_bank + 1) * w]
+                cols = slice(t * P, (t + 1) * P)
+                nc.tensor.matmul_mx(
+                    out=enc_banks[c, g, t],
+                    lhsT=we_codes[:, g, cols].bitcast(X4), lhsT_scale=we_scales[:, g, cols],
+                    rhs=r_codes[c][:, :w].bitcast(X4), rhs_scale=r_scales[c][:, :w], start=True, stop=True)
 
-        def eo(c, g, b):
+        def add_z_theta(c, g, t):
+            w = CHUNKS[c]
+            if t == 0:
+                shifted[c, g] = work.tile([P, 4, WIDEST], F32, name="shifted")
+            z_t = z_words[c][:, g, t // 2, :w].bitcast(BF16).rearrange("p (r e) -> p r e", e=2)[:, :, t % 2]
+            nc.vector.scalar_tensor_tensor(out=shifted[c, g][:, t, :w], in0=enc_banks[c, g, t],
+                                           scalar=theta_sb[:, g, t:t + 1], in1=z_t, op0=ALU.add, op1=ALU.add)
+
+        def relu_part(c, g, t):
+            w = CHUNKS[c]
+            if t == 0:
+                upper[c, g] = work.tile([P, 4, WIDEST], F32, name="upper")
+            if (c, g) == (LAST, 0):
+                nc.vector.tensor_scalar(out=upper[c, g][:, t, :w], in0=shifted[c, g][:, t, :w],
+                                        scalar1=minus_2theta[:, g, t:t + 1], scalar2=0.0, op0=ALU.add, op1=ALU.max)
+            else:
+                nc.scalar.activation(out=upper[c, g][:, t, :w], in_=shifted[c, g][:, t, :w], func=ACT.Relu,
+                                     bias=minus_2theta[:, g, t:t + 1])
+
+        def add_and_relu(c, g):
+            for t in range(4):
+                add_z_theta(c, g, t)
+                relu_part(c, g, t)
+
+        def combine(c, g):
+            half = CHUNKS[c] // 2
+            result[c, g] = work.tile([P, 2, 4, WIDEST // 2], F32, name="result")
+            for h in range(2):
+                tokens = slice(h * half, (h + 1) * half)
+                nc.vector.scalar_tensor_tensor(out=result[c, g][:, h, :, :half], in0=shifted[c, g][:, :, tokens],
+                                               scalar=0.0, in1=upper[c, g][:, :, tokens], op0=ALU.min, op1=ALU.add)
+
+        def gpsimd_copy(out, in_):
+            nc.gpsimd.tensor_scalar(out=out, in0=in_, scalar1=1.0, scalar2=0.0, op0=ALU.mult, op1=ALU.add)
+
+        def round_result(c, g, first, second):
+            half = CHUNKS[c] // 2
+            if (c, g) != (LAST, 1):
+                rounded[c, g] = work.tile([P, 4 * WIDEST], BF16, name="rounded", bufs=3, align_bytes=64)
+            home = rounded[LAST, 0][:, 4 * CHUNKS[LAST]:] if (c, g) == (LAST, 1) else rounded[c, g][:]
+            for h, copy in enumerate((first, second)):
+                copy(out=home[:, 4 * half * h:4 * half * (h + 1)].rearrange("p (r t) -> p r t", t=4),
+                     in_=result[c, g][:, h, :, :half].rearrange("p t r -> p r t"))
+
+        def quantise_result(c, g):
+            w = CHUNKS[c]
+            tokens = slice(STARTS[c], STARTS[c] + w)
+            codes = work.tile([P, WIDEST], U32, name="out_codes", bufs=3, align_bytes=64)
+            quantise(codes[:, :w], early_scales[:, g, tokens], rounded[c, g][:, :4 * w])
+            nc.sync.dma_start(out=out_1[g].rearrange("p m t -> p (m t)").bitcast(I32)[:, tokens],
+                              in_=codes[:, :w].bitcast(I32))
+
+        def quantise_last_result():
+            codes = work.tile([P, WIDEST], U32, name="out_codes", bufs=3, align_bytes=64)
+            quantise(codes[:], last_scales[:].rearrange("p g m -> p (g m)"), rounded[LAST, 0][:])
+            nc.sync.dma_start(out=out_1.rearrange("g p m t -> p g (m t)").bitcast(I32)[:, :, STARTS[LAST]:S],
+                              in_=codes[:].bitcast(I32).rearrange("p (g m) -> p g m", g=2))
+
+        def turn_back(c, g, b):
+            per_half = CHUNKS[c] // 2 // P
+            back_banks[c, g, b] = bank()
+            tokens = slice((b % per_half) * P, (b % per_half + 1) * P)
+            for t in range(4):
+                nc.tensor.transpose(back_banks[c, g, b][:, t * P:(t + 1) * P],
+                                    result[c, g][:, b // per_half, t, tokens], ident[:])
+
+        def store_rows(c, g, b):
             if b % 2 == 0:
-                rest[c, g, b // 2] = work.tile([P, 2, 512], F32, name="res", bufs=5)
-            res = rest[c, g, b // 2]
-            copy = nc.vector.tensor_copy if (c, g, b) in EOV else nc.scalar.copy
-            copy(out=res[:, b % 2, :].rearrange("p (m t) -> p m t", t=4),
-                 in_=obank[c, g, b][:].rearrange("p (t m) -> p m t", t=4))
-            r0 = starts[c] + b * P
-            if c == n - 1:
-                nc.sync.dma_start(out=out_0[r0:r0 + P, g * 512:(g + 1) * 512], in_=res[:, b % 2, :])
+                rows[c, g, b // 2] = work.tile([P, 2, GROUP], F32, name="rows", bufs=5)
+            pair = rows[c, g, b // 2]
+            nc.scalar.copy(out=pair[:, b % 2, :].rearrange("p (m t) -> p m t", t=4),
+                           in_=back_banks[c, g, b][:].rearrange("p (t m) -> p m t", t=4))
+            row0 = STARTS[c] + b * P
+            atoms = slice(g * GROUP, (g + 1) * GROUP)
+            if (c, g) == (LAST, 1):
+                nc.sync.dma_start(out=out_0[row0:row0 + P, atoms], in_=pair[:, b % 2, :])
             elif b % 2 == 1:
-                nc.sync.dma_start(
-                    out=out_0[r0 - P:r0 + P, g * 512:(g + 1) * 512].rearrange("(b p) x -> p b x", p=P), in_=res[:])
+                nc.sync.dma_start(out=out_0[row0 - P:row0 + P, atoms].rearrange("(b p) x -> p b x", p=P), in_=pair[:])
 
-        def il(name, g, q):
-            raw = (dic_raw if name == "d" else we_raw)[g]
-            if (name, g) not in grp:
-                grp[name, g] = work.tile([P, 2048], BF16, name="grouped", bufs=3, align_bytes=64)
-            dst = grp[name, g][:].rearrange("p (t m j) -> p t m j", t=4, j=4)[:, 2 * q:2 * q + 2]
-            src = raw[:].rearrange("p j (m t) -> p t m j", t=4)[:, 2 * q:2 * q + 2]
-            copy = nc.vector.tensor_copy if IL[name, g, q] == "v" else nc.scalar.copy
-            copy(out=dst, in_=src)
+        def turn_back_and_store(c, g):
+            for b in blocks(c):
+                turn_back(c, g, b)
+                store_rows(c, g, b)
 
-        def qw(name, g):
-            codes, scales = (dic_c, dic_s) if name == "d" else (we_c, we_s)
-            quant(codes[:, g, :], scales[:, g, :], grp[name, g][:])
-
-        def store_scales(part, m0, m1):
+        def store_scales(scales, m0, m1):
             for q in range(4):
                 nc.sync.dma_start(
                     out=out_2.bitcast(I32)[:, 4 * q:4 * q + 4, m0 // 4:m1 // 4].rearrange("g r m -> r g m"),
-                    in_=out_s[part][:].bitcast(I32)[32 * q:32 * q + 4, :, :])
+                    in_=scales[:].bitcast(I32)[32 * q:32 * q + 4, :, :])
 
-        def ss(part):
-            store_scales(part, 0 if part == 0 else early, early if part == 0 else S)
+        on_vector, on_scalar = nc.vector.tensor_copy, nc.scalar.copy
 
-        steps = {"tz": tz, "za": za_, "ez": ez, "qz": qz, "tk": tk, "ek": ek, "mm1": mm1, "rs": res_, "qr": qr,
-                 "mm2": mm2, "p1": p1, "relu": relu, "p3": p3, "cast": cast, "qo": qo, "to": to, "eo": eo,
-                 "ev": ev, "evp": evp, "tr": tr, "il": il, "qw": qw, "ss": ss}
-        for step in ORDER:
-            steps[step[0]](*step[1:])
+        turn_z(0, 0)
+        warm_up(WARM_UP[0])
+        scale_z(0, 0, 0)
+        scale_z(0, 0, 1)
+        dic_laid = [lay_out_weight(dic_raw[0], on_scalar, on_vector), lay_out_weight(dic_raw[1], on_vector, on_scalar)]
+        turn_k(0)
+        warm_up(WARM_UP[1])
+        quantise(dic_codes[:, 0, :], dic_scales[:, 0, :], dic_laid[0][:])
+        quantise_za(0)
+        quantise(dic_codes[:, 1, :], dic_scales[:, 1, :], dic_laid[1][:])
+        reconstruct(0)
+        we_laid = [lay_out_weight(we_raw[0], on_vector, on_scalar)]
+        keep_z(0, 0, 0)
+        keep_z(0, 0, 1)
+        turn_z(1, 0)
+        subtract_from_k(0)
+        quantise(we_codes[:, 0, :], we_scales[:, 0, :], we_laid[0][:])
+        quantise_resid(0)
+        we_laid.append(lay_out_weight(we_raw[1], on_scalar, on_scalar))
+        encode(0, 0)
+        scale_and_keep_z(1, 0)
+
+        for c in range(LAST):
+            before_last = c == LAST - 1
+            z_pieces = pieces(c + 1)[1:] if c == 0 else pieces(c + 1)
+            for h in z_pieces:
+                turn_z(c + 1, h)
+            add_and_relu(c, 0)
+            if c == 0:
+                turn_k(1)
+            for h in z_pieces:
+                scale_and_keep_z(c + 1, h)
+            if c == 0:
+                quantise(we_codes[:, 1, :], we_scales[:, 1, :], we_laid[1][:])
+            else:
+                turn_back_and_store(c - 1, 1)
+            quantise_za(c + 1)
+            if c > 0 and not before_last:
+                quantise_result(c - 1, 1)
+            encode(c, 1)
+            reconstruct(c + 1)
+            combine(c, 0)
+            if before_last:
+                quantise_result(c - 1, 1)
+            round_result(c, 0, gpsimd_copy, on_scalar if before_last else gpsimd_copy)
+            add_and_relu(c, 1)
+            turn_back_and_store(c, 0)
+            subtract_from_k(c + 1)
+            quantise_result(c, 0)
+            quantise_resid(c + 1)
+            if not before_last:
+                turn_k(c + 2)
+            encode(c + 1, 0)
+            combine(c, 1)
+            round_result(c, 1, on_scalar if before_last else gpsimd_copy, gpsimd_copy)
+
+        encode(LAST, 1)
+        for g in range(2):
+            for b in (2 * g, 2 * g + 1):
+                turn_back(LAST - 1, 1, b)
+            for b in (2 * g, 2 * g + 1):
+                store_rows(LAST - 1, 1, b)
+            for t in range(4):
+                add_z_theta(LAST, g, t)
+        for g in range(2):
+            for t in range(4):
+                relu_part(LAST, g, t)
+        combine(LAST, 0)
+        quantise_result(LAST - 1, 1)
+        store_scales(early_scales, 0, STARTS[LAST])
+        turn_back_and_store(LAST, 0)
+        combine(LAST, 1)
+        turn_back_and_store(LAST, 1)
+        round_result(LAST, 0, on_vector, on_vector)
+        round_result(LAST, 1, on_vector, on_vector)
+        quantise_last_result()
+        store_scales(last_scales, STARTS[LAST], S)

@@ -44,6 +44,8 @@ def tile_dictionarykvcachelistastep_x1_kernel(tc, k, z, a, dic, we, theta, out_0
 
         ident = keep.tile([P, P], F32, name="ident")
         make_identity(nc, ident[:])
+        ident_bf16 = keep.tile([P, P], BF16, name="ident_bf16")
+        make_identity(nc, ident_bf16[:])
 
         a_sb = keep.tile([P, 2, 4], BF16, name="a_sb")
         theta_sb = keep.tile([P, 2, 4], BF16, name="theta_sb")
@@ -86,7 +88,7 @@ def tile_dictionarykvcachelistastep_x1_kernel(tc, k, z, a, dic, we, theta, out_0
         last_scales = keep.tile([P, 2, CHUNKS[LAST]], U8, name="last_scales", align_bytes=64)
 
         z_banks, z_words, za, za_codes, za_scales = {}, {}, {}, {}, {}
-        k_words, recon_banks, r_codes, r_scales, resid = {}, {}, {}, {}, {}
+        k_words, recon_banks, negated, resid_banks, resid, r_codes, r_scales = {}, {}, {}, {}, {}, {}, {}
         enc_banks, shifted, upper, result, rounded, back_banks, rows = {}, {}, {}, {}, {}, {}, {}
 
         def pieces(c):
@@ -94,6 +96,9 @@ def tile_dictionarykvcachelistastep_x1_kernel(tc, k, z, a, dic, we, theta, out_0
 
         def blocks(c):
             return range(CHUNKS[c] // P)
+
+        def on_tensor_road(c, h):
+            return CHUNKS[c] == WIDEST and h == 0
 
         def quantise(codes, scales, src):
             nc.vector.quantize_mx(out=codes.bitcast(X4), scales=scales, in_=src)
@@ -144,43 +149,69 @@ def tile_dictionarykvcachelistastep_x1_kernel(tc, k, z, a, dic, we, theta, out_0
                 scale_z(c, h, g)
                 keep_z(c, h, g)
 
-        def quantise_za(c):
-            w = CHUNKS[c]
-            za_codes[c] = work.tile([P, 2, WIDEST], U32, name="za_codes", align_bytes=64)
-            za_scales[c] = work.tile([P, 2, WIDEST], U8, name="za_scales", align_bytes=64)
+        def quantise_za(c, h):
+            if h == 0:
+                za_codes[c] = work.tile([P, 2, WIDEST], U32, name="za_codes", align_bytes=64)
+                za_scales[c] = work.tile([P, 2, WIDEST], U8, name="za_scales", align_bytes=64)
+            tokens = slice(h * PIECE, (h + 1) * PIECE)
             for g in range(2):
-                quantise(za_codes[c][:, g, :w], za_scales[c][:, g, :w], za[c][:, g, :4 * w])
+                quantise(za_codes[c][:, g, tokens], za_scales[c][:, g, tokens],
+                         za[c][:, g, 4 * h * PIECE:4 * (h + 1) * PIECE])
 
         def turn_k(c):
-            turned = [transpose_words(k_sb[STARTS[c] // PIECE + h], 0) for h in pieces(c)]
-            k_words[c] = work.tile([P, WIDEST, 2], F32, name="k_words")
-            for h in pieces(c):
-                nc.scalar.copy(out=k_words[c][:, h * PIECE:(h + 1) * PIECE, :],
-                               in_=turned[h][:].rearrange("p (u r) -> p r u", u=2))
+            turned = transpose_words(k_sb[STARTS[c] // PIECE + pieces(c)[-1]], 0)
+            k_words[c] = work.tile([P, PIECE, 2], F32, name="k_words")
+            nc.scalar.copy(out=k_words[c][:], in_=turned[:].rearrange("p (u r) -> p r u", u=2))
 
-        def reconstruct(c):
-            for b in blocks(c):
+        def reconstruct(c, h):
+            for b in (2 * h, 2 * h + 1):
                 recon_banks[c, b] = bank()
                 tokens = slice(b * P, (b + 1) * P)
-                for t in range(4):
-                    cols = slice(t * P, (t + 1) * P)
+                if on_tensor_road(c, h):
                     for g in range(2):
                         nc.tensor.matmul_mx(
-                            out=recon_banks[c, b][:, cols],
-                            lhsT=dic_codes[:, g, cols].bitcast(X4), lhsT_scale=dic_scales[:, g, cols],
-                            rhs=za_codes[c][:, g, tokens].bitcast(X4), rhs_scale=za_scales[c][:, g, tokens],
+                            out=recon_banks[c, b][:],
+                            lhsT=za_codes[c][:, g, tokens].bitcast(X4), lhsT_scale=za_scales[c][:, g, tokens],
+                            rhs=dic_codes[:, g, :].bitcast(X4), rhs_scale=dic_scales[:, g, :],
                             start=(g == 0), stop=(g == 1))
+                else:
+                    for t in range(4):
+                        cols = slice(t * P, (t + 1) * P)
+                        for g in range(2):
+                            nc.tensor.matmul_mx(
+                                out=recon_banks[c, b][:, cols],
+                                lhsT=dic_codes[:, g, cols].bitcast(X4), lhsT_scale=dic_scales[:, g, cols],
+                                rhs=za_codes[c][:, g, tokens].bitcast(X4), rhs_scale=za_scales[c][:, g, tokens],
+                                start=(g == 0), stop=(g == 1))
 
-        def subtract_from_k(c):
+        def negate_recon(c):
+            for b in range(2):
+                negated[c, b] = work.tile([P, DK], F32, name="negated")
+                nc.scalar.mul(out=negated[c, b][:], in_=recon_banks[c, b][:], mul=-1.0)
+
+        def sum_resid_on_tensor(c):
+            for b in range(2):
+                resid_banks[c, b] = bank()
+                for t in range(4):
+                    nc.tensor.matmul(resid_banks[c, b][:, t * P:(t + 1) * P],
+                                     lhsT=k_sb[STARTS[c] // PIECE][:, b, t:DK:4], rhs=ident_bf16[:],
+                                     start=(t == 0), stop=False)
+                for t in range(4):
+                    nc.tensor.matmul(resid_banks[c, b][:, t * P:(t + 1) * P],
+                                     lhsT=negated[c, b][:, t * P:(t + 1) * P], rhs=ident[:],
+                                     start=False, stop=(t == 3), is_transpose=True)
+
+        def round_resid(c):
             resid[c] = work.tile([P, 4 * WIDEST], BF16, name="resid", bufs=1, align_bytes=64)
-            k_turned = k_words[c][:].rearrange("p r u -> p (r u)").bitcast(BF16)
+            k_turned = k_words[c][:].rearrange("p r u -> p (r u)").bitcast(BF16).rearrange("p (r t) -> p r t", t=4)
             for b in blocks(c):
-                cols = slice(b * 4 * P, (b + 1) * 4 * P)
-                nc.vector.tensor_tensor(
-                    out=resid[c][:, cols].rearrange("p (r t) -> p r t", t=4),
-                    in0=k_turned[:, cols].rearrange("p (r t) -> p r t", t=4),
-                    in1=recon_banks[c, b][:].rearrange("p (t r) -> p r t", t=4),
-                    op=ALU.subtract)
+                dst = resid[c][:, b * 4 * P:(b + 1) * 4 * P].rearrange("p (r t) -> p r t", t=4)
+                if on_tensor_road(c, b // 2):
+                    nc.scalar.copy(out=dst, in_=resid_banks[c, b][:].rearrange("p (t r) -> p r t", t=4))
+                else:
+                    nc.vector.tensor_tensor(out=dst, in0=k_turned[:, (b % 2) * P:(b % 2 + 1) * P, :],
+                                            in1=recon_banks[c, b][:].rearrange("p (t r) -> p r t", t=4),
+                                            op=ALU.subtract)
 
         def quantise_resid(c):
             w = CHUNKS[c]
@@ -225,25 +256,33 @@ def tile_dictionarykvcachelistastep_x1_kernel(tc, k, z, a, dic, we, theta, out_0
                 add_z_theta(c, g, t)
                 relu_part(c, g, t)
 
-        def combine(c, g):
+        def combine_half(c, g, h):
             half = CHUNKS[c] // 2
-            result[c, g] = work.tile([P, 2, 4, WIDEST // 2], F32, name="result")
+            if h == 0:
+                result[c, g] = work.tile([P, 2, 4, WIDEST // 2], F32, name="result")
+            tokens = slice(h * half, (h + 1) * half)
+            nc.vector.scalar_tensor_tensor(out=result[c, g][:, h, :, :half], in0=shifted[c, g][:, :, tokens],
+                                           scalar=0.0, in1=upper[c, g][:, :, tokens], op0=ALU.min, op1=ALU.add)
+
+        def combine(c, g):
             for h in range(2):
-                tokens = slice(h * half, (h + 1) * half)
-                nc.vector.scalar_tensor_tensor(out=result[c, g][:, h, :, :half], in0=shifted[c, g][:, :, tokens],
-                                               scalar=0.0, in1=upper[c, g][:, :, tokens], op0=ALU.min, op1=ALU.add)
+                combine_half(c, g, h)
 
         def gpsimd_copy(out, in_):
             nc.gpsimd.tensor_scalar(out=out, in0=in_, scalar1=1.0, scalar2=0.0, op0=ALU.mult, op1=ALU.add)
 
-        def round_result(c, g, first, second):
-            half = CHUNKS[c] // 2
+        def round_result(c, g, copies):
+            w = CHUNKS[c]
             if (c, g) != (LAST, 1):
                 rounded[c, g] = work.tile([P, 4 * WIDEST], BF16, name="rounded", bufs=3, align_bytes=64)
-            home = rounded[LAST, 0][:, 4 * CHUNKS[LAST]:] if (c, g) == (LAST, 1) else rounded[c, g][:]
-            for h, copy in enumerate((first, second)):
-                copy(out=home[:, 4 * half * h:4 * half * (h + 1)].rearrange("p (r t) -> p r t", t=4),
-                     in_=result[c, g][:, h, :, :half].rearrange("p t r -> p r t"))
+            home = rounded[LAST, 0][:, 4 * w:] if (c, g) == (LAST, 1) else rounded[c, g][:, :4 * w]
+            dst = home.rearrange("p (h r t) -> p h r t", h=2, t=4)
+            src = result[c, g][:, :, :, :w // 2].rearrange("p h t r -> p h r t")
+            if len(copies) == 1:
+                copies[0](out=dst, in_=src)
+            else:
+                for h in range(2):
+                    copies[h](out=dst[:, h], in_=src[:, h])
 
         def quantise_result(c, g):
             w = CHUNKS[c]
@@ -301,53 +340,79 @@ def tile_dictionarykvcachelistastep_x1_kernel(tc, k, z, a, dic, we, theta, out_0
         turn_k(0)
         warm_up(WARM_UP[1])
         quantise(dic_codes[:, 0, :], dic_scales[:, 0, :], dic_laid[0][:])
-        quantise_za(0)
+        quantise_za(0, 0)
         quantise(dic_codes[:, 1, :], dic_scales[:, 1, :], dic_laid[1][:])
-        reconstruct(0)
+        reconstruct(0, 0)
         we_laid = [lay_out_weight(we_raw[0], on_vector, on_scalar)]
         keep_z(0, 0, 0)
         keep_z(0, 0, 1)
         turn_z(1, 0)
-        subtract_from_k(0)
+        round_resid(0)
         quantise(we_codes[:, 0, :], we_scales[:, 0, :], we_laid[0][:])
         quantise_resid(0)
         we_laid.append(lay_out_weight(we_raw[1], on_scalar, on_scalar))
         encode(0, 0)
         scale_and_keep_z(1, 0)
 
-        for c in range(LAST):
-            before_last = c == LAST - 1
-            z_pieces = pieces(c + 1)[1:] if c == 0 else pieces(c + 1)
-            for h in z_pieces:
-                turn_z(c + 1, h)
-            add_and_relu(c, 0)
+        for c in range(LAST - 1):
             if c == 0:
+                turn_z(1, 1)
+                add_and_relu(0, 0)
                 turn_k(1)
-            for h in z_pieces:
-                scale_and_keep_z(c + 1, h)
-            if c == 0:
+                quantise_za(1, 0)
+                reconstruct(1, 0)
+                scale_and_keep_z(1, 1)
                 quantise(we_codes[:, 1, :], we_scales[:, 1, :], we_laid[1][:])
             else:
+                turn_z(c + 1, 0)
+                turn_z(c + 1, 1)
+                add_and_relu(c, 0)
+                scale_and_keep_z(c + 1, 0)
+                scale_z(c + 1, 1, 0)
+                keep_z(c + 1, 1, 0)
+                quantise_za(c + 1, 0)
+                scale_z(c + 1, 1, 1)
+                keep_z(c + 1, 1, 1)
                 turn_back_and_store(c - 1, 1)
-            quantise_za(c + 1)
-            if c > 0 and not before_last:
+                reconstruct(c + 1, 0)
                 quantise_result(c - 1, 1)
+            quantise_za(c + 1, 1)
             encode(c, 1)
-            reconstruct(c + 1)
+            negate_recon(c + 1)
+            reconstruct(c + 1, 1)
+            sum_resid_on_tensor(c + 1)
             combine(c, 0)
-            if before_last:
-                quantise_result(c - 1, 1)
-            round_result(c, 0, gpsimd_copy, on_scalar if before_last else gpsimd_copy)
+            round_result(c, 0, [gpsimd_copy])
             add_and_relu(c, 1)
+            round_resid(c + 1)
             turn_back_and_store(c, 0)
-            subtract_from_k(c + 1)
             quantise_result(c, 0)
+            combine_half(c, 1, 0)
             quantise_resid(c + 1)
-            if not before_last:
-                turn_k(c + 2)
+            turn_k(c + 2)
             encode(c + 1, 0)
-            combine(c, 1)
-            round_result(c, 1, on_scalar if before_last else gpsimd_copy, gpsimd_copy)
+            combine_half(c, 1, 1)
+            round_result(c, 1, [gpsimd_copy])
+
+        c = LAST - 1
+        turn_z(LAST, 0)
+        add_and_relu(c, 0)
+        scale_and_keep_z(LAST, 0)
+        turn_back_and_store(c - 1, 1)
+        quantise_za(LAST, 0)
+        encode(c, 1)
+        reconstruct(LAST, 0)
+        combine(c, 0)
+        quantise_result(c - 1, 1)
+        round_result(c, 0, [gpsimd_copy, on_scalar])
+        add_and_relu(c, 1)
+        turn_back_and_store(c, 0)
+        round_resid(LAST)
+        quantise_result(c, 0)
+        quantise_resid(LAST)
+        encode(LAST, 0)
+        combine(c, 1)
+        round_result(c, 1, [on_scalar, gpsimd_copy])
 
         encode(LAST, 1)
         for g in range(2):
@@ -366,7 +431,7 @@ def tile_dictionarykvcachelistastep_x1_kernel(tc, k, z, a, dic, we, theta, out_0
         turn_back_and_store(LAST, 0)
         combine(LAST, 1)
         turn_back_and_store(LAST, 1)
-        round_result(LAST, 0, on_vector, on_vector)
-        round_result(LAST, 1, on_vector, on_vector)
+        round_result(LAST, 0, [on_vector, on_vector])
+        round_result(LAST, 1, [on_vector, on_vector])
         quantise_last_result()
         store_scales(last_scales, STARTS[LAST], S)

@@ -24,7 +24,7 @@ CHUNKS = [256, 512, 512, 512, 256]
 WIDEST = max(CHUNKS)
 LAST = len(CHUNKS) - 1
 STARTS = [sum(CHUNKS[:c]) for c in range(len(CHUNKS))]
-WARM_UP = (4, 5)
+WARM_UP = (3, 3)
 
 
 def tile_dictionarykvcachelistastep_x1_kernel(tc, k, z, a, dic, we, theta, out_0, out_1, out_2):
@@ -244,7 +244,7 @@ def tile_dictionarykvcachelistastep_x1_kernel(tc, k, z, a, dic, we, theta, out_0
             w = CHUNKS[c]
             if t == 0:
                 upper[c, g] = work.tile([P, 4, WIDEST], F32, name="upper")
-            if (c, g) == (LAST, 0):
+            if c == LAST and (g == 0 or t >= 2):
                 nc.vector.tensor_scalar(out=upper[c, g][:, t, :w], in0=shifted[c, g][:, t, :w],
                                         scalar1=minus_2theta[:, g, t:t + 1], scalar2=0.0, op0=ALU.add, op1=ALU.max)
             else:
@@ -404,7 +404,7 @@ def tile_dictionarykvcachelistastep_x1_kernel(tc, k, z, a, dic, we, theta, out_0
         reconstruct(LAST, 0)
         combine(c, 0)
         quantise_result(c - 1, 1)
-        round_result(c, 0, [gpsimd_copy, on_scalar])
+        round_result(c, 0, [gpsimd_copy])
         add_and_relu(c, 1)
         turn_back_and_store(c, 0)
         round_resid(LAST)

from contextlib import ExitStack

import concourse.mybir as mybir
from concourse.masks import make_identity

S, A, DK = 2048, 1024, 512
FLOPS = 4 * S * A * DK

F32 = mybir.dt.float32
BF16 = mybir.dt.bfloat16
U32 = mybir.dt.uint32
I32 = mybir.dt.int32
U8 = mybir.dt.uint8
X4 = mybir.dt.float8_e4m3fn_x4
ALU = mybir.AluOpType
ACT = mybir.ActivationFunctionType

P = 128
GROUP = 512
BANK = 512
BANKS = 8
PIECE = 256
CHUNKS = [256, 512, 512, 512, 256]
WIDEST = max(CHUNKS)
LAST = len(CHUNKS) - 1
STARTS = [sum(CHUNKS[:c]) for c in range(len(CHUNKS))]
WARM_UP = (3, 3)


def tile_dictionarykvcachelistastep_x1_kernel(tc, k, z, a, dic, we, theta, out_0, out_1, out_2):
    nc = tc.nc

    with ExitStack() as ctx:
        keep = ctx.enter_context(tc.tile_pool(name="keep", bufs=1))
        work = ctx.enter_context(tc.tile_pool(name="work", bufs=2))
        psum = ctx.enter_context(tc.psum_pool(name="psum", bufs=1))
        ctx.enter_context(tc.manual_schedule())

        taken = []

        def bank():
            taken.append(len(taken) % BANKS)
            return psum.tile([P, BANK], F32, name="bank%d" % taken[-1])

        ident = keep.tile([P, P], F32, name="ident")
        make_identity(nc, ident[:])
        ident_bf16 = keep.tile([P, P], BF16, name="ident_bf16")
        make_identity(nc, ident_bf16[:])

        a_sb = keep.tile([P, 2, 4], BF16, name="a_sb")
        theta_sb = keep.tile([P, 2, 4], BF16, name="theta_sb")
        minus_2theta = keep.tile([P, 2, 4], F32, name="minus_2theta")
        nc.scalar.dma_start(out=a_sb[:], in_=a.rearrange("(g p t) -> p g t", g=2, t=4))
        nc.scalar.dma_start(out=theta_sb[:], in_=theta.rearrange("(g p t) -> p g t", g=2, t=4))

        z_sb = [keep.tile([P, 2, A], BF16, name="z%d" % j) for j in range(S // PIECE)]
        k_sb = [keep.tile([P, 2, DK], BF16, name="k%d" % j) for j in range(S // PIECE)]
        dic_raw = [keep.tile([P, 4, DK], BF16, name="dic_raw%d" % g) for g in range(2)]
        we_raw = [keep.tile([P, 4, GROUP], BF16, name="we_raw%d" % g) for g in range(2)]

        def load_tokens(tiles, src, j):
            nc.sync.dma_start(out=tiles[j][:], in_=src[j * PIECE:(j + 1) * PIECE, :].rearrange("(b p) x -> p b x", p=P))

        def load_weight(tile, src):
            nc.sync.dma_start(out=tile[:], in_=src.rearrange("(p j) x -> p j x", j=4))

        load_tokens(z_sb, z, 0)
        load_weight(dic_raw[0], dic[0:GROUP, :])
        load_weight(dic_raw[1], dic[GROUP:A, :])
        load_tokens(k_sb, k, 0)
        load_weight(we_raw[0], we[:, 0:GROUP])
        load_tokens(z_sb, z, 1)
        load_weight(we_raw[1], we[:, GROUP:A])
        load_tokens(z_sb, z, 2)
        load_tokens(k_sb, k, 1)
        load_tokens(k_sb, k, 2)
        for j in range(3, S // PIECE):
            load_tokens(z_sb, z, j)
            load_tokens(k_sb, k, j)

        nc.scalar.mul(out=minus_2theta[:], in_=theta_sb[:], mul=-2.0)

        dic_codes = keep.tile([P, 2, DK], U32, name="dic_codes", align_bytes=64)
        dic_scales = keep.tile([P, 2, DK], U8, name="dic_scales", align_bytes=64)
        we_codes = keep.tile([P, 2, GROUP], U32, name="we_codes", align_bytes=64)
        we_scales = keep.tile([P, 2, GROUP], U8, name="we_scales", align_bytes=64)
        early_scales = keep.tile([P, 2, STARTS[LAST]], U8, name="early_scales", align_bytes=64)
        last_scales = keep.tile([P, 2, CHUNKS[LAST]], U8, name="last_scales", align_bytes=64)

        z_banks, z_words, za, za_codes, za_scales = {}, {}, {}, {}, {}
        k_words, recon_banks, negated, resid_banks, resid, r_codes, r_scales = {}, {}, {}, {}, {}, {}, {}
        enc_banks, shifted, upper, result, rounded, back_banks, rows = {}, {}, {}, {}, {}, {}, {}

        def pieces(c):
            return range(CHUNKS[c] // PIECE)

        def blocks(c):
            return range(CHUNKS[c] // P)

        def on_tensor_road(c, h):
            return CHUNKS[c] == WIDEST and h == 0

        def quantise(codes, scales, src):
            nc.vector.quantize_mx(out=codes.bitcast(X4), scales=scales, in_=src)

        def lay_out_weight(raw, first, second):
            laid = work.tile([P, 4 * GROUP], BF16, name="laid", bufs=3, align_bytes=64)
            dst = laid[:].rearrange("p (t m j) -> p t m j", t=4, j=4)
            src = raw[:].rearrange("p j (m t) -> p t m j", t=4)
            first(out=dst[:, 0:2], in_=src[:, 0:2])
            second(out=dst[:, 2:4], in_=src[:, 2:4])
            return laid

        def warm_up(count):
            unread = bank()
            for j in range(count):
                nc.tensor.matmul(unread[:], lhsT=z_sb[0][:, 0, 0:P], rhs=z_sb[0][:, 0, 0:BANK], start=True, stop=True)

        def transpose_words(src, word0):
            turned = bank()
            words = src[:].bitcast(F32)
            for b in range(2):
                for u in range(2):
                    nc.tensor.transpose(turned[:, u * PIECE + b * P:u * PIECE + (b + 1) * P],
                                        words[:, b, word0 + u:word0 + GROUP // 2:2], ident[:])
            return turned

        def turn_z(c, h):
            for g in range(2):
                z_banks[c, h, g] = transpose_words(z_sb[STARTS[c] // PIECE + h], g * GROUP // 2)

        def scale_z(c, h, g):
            if c not in za:
                za[c] = work.tile([P, 2, 4 * WIDEST], BF16, name="za", bufs=1, align_bytes=64)
            nc.vector.tensor_tensor(
                out=za[c][:, g, h * 4 * PIECE:(h + 1) * 4 * PIECE].rearrange("p (r u e) -> p r u e", u=2, e=2),
                in0=z_banks[c, h, g][:].bitcast(BF16).rearrange("p (u r e) -> p r u e", u=2, e=2),
                in1=a_sb[:, g:g + 1, :].rearrange("p o (u e) -> p o u e", u=2).to_broadcast([P, PIECE, 2, 2]),
                op=ALU.mult)

        def keep_z(c, h, g):
            if c not in z_words:
                z_words[c] = work.tile([P, 2, 2, WIDEST], F32, name="z_words")
            nc.scalar.copy(out=z_words[c][:, g, :, h * PIECE:(h + 1) * PIECE],
                           in_=z_banks[c, h, g][:].rearrange("p (u r) -> p u r", u=2))

        def scale_and_keep_z(c, h):
            for g in range(2):
                scale_z(c, h, g)
                keep_z(c, h, g)

        def quantise_za(c, h):
            if h == 0:
                za_codes[c] = work.tile([P, 2, WIDEST], U32, name="za_codes", align_bytes=64)
                za_scales[c] = work.tile([P, 2, WIDEST], U8, name="za_scales", align_bytes=64)
            tokens = slice(h * PIECE, (h + 1) * PIECE)
            for g in range(2):
                quantise(za_codes[c][:, g, tokens], za_scales[c][:, g, tokens],
                         za[c][:, g, 4 * h * PIECE:4 * (h + 1) * PIECE])

        def turn_k(c):
            turned = transpose_words(k_sb[STARTS[c] // PIECE + pieces(c)[-1]], 0)
            k_words[c] = work.tile([P, PIECE, 2], F32, name="k_words")
            nc.scalar.copy(out=k_words[c][:], in_=turned[:].rearrange("p (u r) -> p r u", u=2))

        def reconstruct(c, h):
            for b in (2 * h, 2 * h + 1):
                recon_banks[c, b] = bank()
                tokens = slice(b * P, (b + 1) * P)
                if on_tensor_road(c, h):
                    for g in range(2):
                        nc.tensor.matmul_mx(
                            out=recon_banks[c, b][:],
                            lhsT=za_codes[c][:, g, tokens].bitcast(X4), lhsT_scale=za_scales[c][:, g, tokens],
                            rhs=dic_codes[:, g, :].bitcast(X4), rhs_scale=dic_scales[:, g, :],
                            start=(g == 0), stop=(g == 1))
                else:
                    for t in range(4):
                        cols = slice(t * P, (t + 1) * P)
                        for g in range(2):
                            nc.tensor.matmul_mx(
                                out=recon_banks[c, b][:, cols],
                                lhsT=dic_codes[:, g, cols].bitcast(X4), lhsT_scale=dic_scales[:, g, cols],
                                rhs=za_codes[c][:, g, tokens].bitcast(X4), rhs_scale=za_scales[c][:, g, tokens],
                                start=(g == 0), stop=(g == 1))

        def negate_recon(c):
            for b in range(2):
                negated[c, b] = work.tile([P, DK], F32, name="negated")
                nc.scalar.mul(out=negated[c, b][:], in_=recon_banks[c, b][:], mul=-1.0)

        def sum_resid_on_tensor(c):
            for b in range(2):
                resid_banks[c, b] = bank()
                for t in range(4):
                    nc.tensor.matmul(resid_banks[c, b][:, t * P:(t + 1) * P],
                                     lhsT=k_sb[STARTS[c] // PIECE][:, b, t:DK:4], rhs=ident_bf16[:],
                                     start=(t == 0), stop=False)
                for t in range(4):
                    nc.tensor.matmul(resid_banks[c, b][:, t * P:(t + 1) * P],
                                     lhsT=negated[c, b][:, t * P:(t + 1) * P], rhs=ident[:],
                                     start=False, stop=(t == 3), is_transpose=True)

        def round_resid(c):
            resid[c] = work.tile([P, 4 * WIDEST], BF16, name="resid", bufs=1, align_bytes=64)
            k_turned = k_words[c][:].rearrange("p r u -> p (r u)").bitcast(BF16).rearrange("p (r t) -> p r t", t=4)
            for b in blocks(c):
                dst = resid[c][:, b * 4 * P:(b + 1) * 4 * P].rearrange("p (r t) -> p r t", t=4)
                if on_tensor_road(c, b // 2):
                    nc.scalar.copy(out=dst, in_=resid_banks[c, b][:].rearrange("p (t r) -> p r t", t=4))
                else:
                    nc.vector.tensor_tensor(out=dst, in0=k_turned[:, (b % 2) * P:(b % 2 + 1) * P, :],
                                            in1=recon_banks[c, b][:].rearrange("p (t r) -> p r t", t=4),
                                            op=ALU.subtract)

        def quantise_resid(c):
            w = CHUNKS[c]
            r_codes[c] = work.tile([P, WIDEST], U32, name="r_codes", align_bytes=64)
            r_scales[c] = work.tile([P, WIDEST], U8, name="r_scales", align_bytes=64)
            quantise(r_codes[c][:, :w], r_scales[c][:, :w], resid[c][:, :4 * w])

        def encode(c, g):
            w = CHUNKS[c]
            per_bank = BANK // w
            for t in range(4):
                if t % per_bank == 0:
                    enc = bank()
                enc_banks[c, g, t] = enc[:, (t % per_bank) * w:(t % per_bank + 1) * w]
                cols = slice(t * P, (t + 1) * P)
                nc.tensor.matmul_mx(
                    out=enc_banks[c, g, t],
                    lhsT=we_codes[:, g, cols].bitcast(X4), lhsT_scale=we_scales[:, g, cols],
                    rhs=r_codes[c][:, :w].bitcast(X4), rhs_scale=r_scales[c][:, :w], start=True, stop=True)

        def add_z_theta(c, g, t):
            w = CHUNKS[c]
            if t == 0:
                shifted[c, g] = work.tile([P, 4, WIDEST], F32, name="shifted")
            z_t = z_words[c][:, g, t // 2, :w].bitcast(BF16).rearrange("p (r e) -> p r e", e=2)[:, :, t % 2]
            nc.vector.scalar_tensor_tensor(out=shifted[c, g][:, t, :w], in0=enc_banks[c, g, t],
                                           scalar=theta_sb[:, g, t:t + 1], in1=z_t, op0=ALU.add, op1=ALU.add)

        def relu_part(c, g, t):
            w = CHUNKS[c]
            if t == 0:
                upper[c, g] = work.tile([P, 4, WIDEST], F32, name="upper")
            if c == LAST and (g == 0 or t >= 2):
                nc.vector.tensor_scalar(out=upper[c, g][:, t, :w], in0=shifted[c, g][:, t, :w],
                                        scalar1=minus_2theta[:, g, t:t + 1], scalar2=0.0, op0=ALU.add, op1=ALU.max)
            else:
                nc.scalar.activation(out=upper[c, g][:, t, :w], in_=shifted[c, g][:, t, :w], func=ACT.Relu,
                                     bias=minus_2theta[:, g, t:t + 1])

        def add_and_relu(c, g):
            for t in range(4):
                add_z_theta(c, g, t)
                relu_part(c, g, t)

        def combine_half(c, g, h):
            half = CHUNKS[c] // 2
            if h == 0:
                result[c, g] = work.tile([P, 2, 4, WIDEST // 2], F32, name="result")
            tokens = slice(h * half, (h + 1) * half)
            nc.vector.scalar_tensor_tensor(out=result[c, g][:, h, :, :half], in0=shifted[c, g][:, :, tokens],
                                           scalar=0.0, in1=upper[c, g][:, :, tokens], op0=ALU.min, op1=ALU.add)

        def combine(c, g):
            for h in range(2):
                combine_half(c, g, h)

        def gpsimd_copy(out, in_):
            nc.gpsimd.tensor_scalar(out=out, in0=in_, scalar1=1.0, scalar2=0.0, op0=ALU.mult, op1=ALU.add)

        def round_result(c, g, copies):
            w = CHUNKS[c]
            if (c, g) != (LAST, 1):
                rounded[c, g] = work.tile([P, 4 * WIDEST], BF16, name="rounded", bufs=3, align_bytes=64)
            home = rounded[LAST, 0][:, 4 * w:] if (c, g) == (LAST, 1) else rounded[c, g][:, :4 * w]
            dst = home.rearrange("p (h r t) -> p h r t", h=2, t=4)
            src = result[c, g][:, :, :, :w // 2].rearrange("p h t r -> p h r t")
            if len(copies) == 1:
                copies[0](out=dst, in_=src)
            else:
                for h in range(2):
                    copies[h](out=dst[:, h], in_=src[:, h])

        def quantise_result(c, g):
            w = CHUNKS[c]
            tokens = slice(STARTS[c], STARTS[c] + w)
            codes = work.tile([P, WIDEST], U32, name="out_codes", bufs=3, align_bytes=64)
            quantise(codes[:, :w], early_scales[:, g, tokens], rounded[c, g][:, :4 * w])
            nc.sync.dma_start(out=out_1[g].rearrange("p m t -> p (m t)").bitcast(I32)[:, tokens],
                              in_=codes[:, :w].bitcast(I32))

        def quantise_last_result():
            codes = work.tile([P, WIDEST], U32, name="out_codes", bufs=3, align_bytes=64)
            quantise(codes[:], last_scales[:].rearrange("p g m -> p (g m)"), rounded[LAST, 0][:])
            nc.sync.dma_start(out=out_1.rearrange("g p m t -> p g (m t)").bitcast(I32)[:, :, STARTS[LAST]:S],
                              in_=codes[:].bitcast(I32).rearrange("p (g m) -> p g m", g=2))

        def turn_back(c, g, b):
            per_half = CHUNKS[c] // 2 // P
            back_banks[c, g, b] = bank()
            tokens = slice((b % per_half) * P, (b % per_half + 1) * P)
            for t in range(4):
                nc.tensor.transpose(back_banks[c, g, b][:, t * P:(t + 1) * P],
                                    result[c, g][:, b // per_half, t, tokens], ident[:])

        def store_rows(c, g, b):
            if b % 2 == 0:
                rows[c, g, b // 2] = work.tile([P, 2, GROUP], F32, name="rows", bufs=5)
            pair = rows[c, g, b // 2]
            nc.scalar.copy(out=pair[:, b % 2, :].rearrange("p (m t) -> p m t", t=4),
                           in_=back_banks[c, g, b][:].rearrange("p (t m) -> p m t", t=4))
            row0 = STARTS[c] + b * P
            atoms = slice(g * GROUP, (g + 1) * GROUP)
            if (c, g) == (LAST, 1):
                nc.sync.dma_start(out=out_0[row0:row0 + P, atoms], in_=pair[:, b % 2, :])
            elif b % 2 == 1:
                nc.sync.dma_start(out=out_0[row0 - P:row0 + P, atoms].rearrange("(b p) x -> p b x", p=P), in_=pair[:])

        def turn_back_and_store(c, g):
            for b in blocks(c):
                turn_back(c, g, b)
                store_rows(c, g, b)

        def store_scales(scales, m0, m1):
            for q in range(4):
                nc.sync.dma_start(
                    out=out_2.bitcast(I32)[:, 4 * q:4 * q + 4, m0 // 4:m1 // 4].rearrange("g r m -> r g m"),
                    in_=scales[:].bitcast(I32)[32 * q:32 * q + 4, :, :])

        on_vector, on_scalar = nc.vector.tensor_copy, nc.scalar.copy

        turn_z(0, 0)
        warm_up(WARM_UP[0])
        scale_z(0, 0, 0)
        scale_z(0, 0, 1)
        dic_laid = [lay_out_weight(dic_raw[0], on_scalar, on_vector), lay_out_weight(dic_raw[1], on_vector, on_scalar)]
        turn_k(0)
        warm_up(WARM_UP[1])
        quantise(dic_codes[:, 0, :], dic_scales[:, 0, :], dic_laid[0][:])
        quantise_za(0, 0)
        quantise(dic_codes[:, 1, :], dic_scales[:, 1, :], dic_laid[1][:])
        reconstruct(0, 0)
        we_laid = [lay_out_weight(we_raw[0], on_vector, on_scalar)]
        keep_z(0, 0, 0)
        keep_z(0, 0, 1)
        turn_z(1, 0)
        round_resid(0)
        quantise(we_codes[:, 0, :], we_scales[:, 0, :], we_laid[0][:])
        quantise_resid(0)
        we_laid.append(lay_out_weight(we_raw[1], on_scalar, on_scalar))
        encode(0, 0)
        scale_and_keep_z(1, 0)

        for c in range(LAST - 1):
            if c == 0:
                turn_z(1, 1)
                add_and_relu(0, 0)
                turn_k(1)
                quantise_za(1, 0)
                reconstruct(1, 0)
                scale_and_keep_z(1, 1)
                quantise(we_codes[:, 1, :], we_scales[:, 1, :], we_laid[1][:])
            else:
                turn_z(c + 1, 0)
                turn_z(c + 1, 1)
                add_and_relu(c, 0)
                scale_and_keep_z(c + 1, 0)
                scale_z(c + 1, 1, 0)
                keep_z(c + 1, 1, 0)
                quantise_za(c + 1, 0)
                scale_z(c + 1, 1, 1)
                keep_z(c + 1, 1, 1)
                turn_back_and_store(c - 1, 1)
                reconstruct(c + 1, 0)
                quantise_result(c - 1, 1)
            quantise_za(c + 1, 1)
            encode(c, 1)
            negate_recon(c + 1)
            reconstruct(c + 1, 1)
            sum_resid_on_tensor(c + 1)
            combine(c, 0)
            round_result(c, 0, [gpsimd_copy])
            add_and_relu(c, 1)
            round_resid(c + 1)
            turn_back_and_store(c, 0)
            quantise_result(c, 0)
            combine_half(c, 1, 0)
            quantise_resid(c + 1)
            turn_k(c + 2)
            encode(c + 1, 0)
            combine_half(c, 1, 1)
            round_result(c, 1, [gpsimd_copy])

        c = LAST - 1
        turn_z(LAST, 0)
        add_and_relu(c, 0)
        scale_and_keep_z(LAST, 0)
        turn_back_and_store(c - 1, 1)
        quantise_za(LAST, 0)
        encode(c, 1)
        reconstruct(LAST, 0)
        combine(c, 0)
        quantise_result(c - 1, 1)
        round_result(c, 0, [gpsimd_copy])
        add_and_relu(c, 1)
        turn_back_and_store(c, 0)
        round_resid(LAST)
        quantise_result(c, 0)
        quantise_resid(LAST)
        encode(LAST, 0)
        combine(c, 1)
        round_result(c, 1, [on_scalar, gpsimd_copy])

        encode(LAST, 1)
        for g in range(2):
            for b in (2 * g, 2 * g + 1):
                turn_back(LAST - 1, 1, b)
            for b in (2 * g, 2 * g + 1):
                store_rows(LAST - 1, 1, b)
            for t in range(4):
                add_z_theta(LAST, g, t)
        for g in range(2):
            for t in range(4):
                relu_part(LAST, g, t)
        combine(LAST, 0)
        quantise_result(LAST - 1, 1)
        store_scales(early_scales, 0, STARTS[LAST])
        turn_back_and_store(LAST, 0)
        combine(LAST, 1)
        turn_back_and_store(LAST, 1)
        round_result(LAST, 0, [on_vector, on_vector])
        round_result(LAST, 1, [on_vector, on_vector])
        quantise_last_result()
        store_scales(last_scales, STARTS[LAST], S)
